import numpy as np
CORES = [12,28,60,100,156,228]
N = 6
W = 256
def setup_inputs(rng):
    amp = 0.5 + 1.5 * rng.random((2, N, 128, 1), dtype=np.float32)
    return {"u": amp[0] * rng.standard_normal((N, 128, W), dtype=np.float32), "b": amp[1] * rng.standard_normal((N, 128, W), dtype=np.float32)}
def setup_inputs_big(rng):
    d = setup_inputs(rng)
    for k in ("u", "b"): d[k] = (d[k].astype(np.float32) * 1024.0).astype(d[k].dtype)
    return d
def setup_inputs_small(rng):
    d = setup_inputs(rng)
    for k in ("u", "b"): d[k] = (d[k].astype(np.float32) * (1 / 1024.0)).astype(d[k].dtype)
    return d
def setup_inputs_apart(rng):
    d = setup_inputs(rng)
    f = (10.0 ** rng.permutation(np.linspace(-1.5, 1.5, N))).astype(np.float32).reshape(N, 1, 1)
    for k in ("u", "b"): d[k] = (d[k].astype(np.float32) * f).astype(d[k].dtype)
    return d
def reference(u, b):
    g = np.concatenate(list(u.astype(np.float64)), axis=1); bb = np.concatenate(list(b.astype(np.float64)), axis=1)
    p = np.concatenate([g[:, -2:], g, g[:, :2]], axis=1)
    n = 0.125 * (p[:, :-4] + p[:, 1:-3] + p[:, 3:-1] + p[:, 4:]) + 0.5 * bb
    d = n - g
    s = np.stack([(d ** 2).mean(axis=1), np.abs(d).max(axis=1)], axis=1)
    return {"y": np.stack([n[:, W * r:W * r + W] for r in range(N)]).astype(np.float32), "s": np.broadcast_to(s.astype(np.float32), (N, 128, 2))}

@@ -1,0 +1,231 @@
+from concourse.bass import DstId, RemoteDMATransfer
+from concourse.mybir import AluOpType
+
+N = 6
+W = 256
+WI = W - 4
+HW = WI // 2
+NSIM = 256
+
+F = "float32"
+SCRATCH = {
+    "U": ("sbuf", [128, W], F), "B": ("sbuf", [128, W], F),
+    "b4": ("sbuf", [128, WI], F), "u8": ("sbuf", [128, WI], F), "D": ("sbuf", [128, WI], F),
+    "ABl": ("sbuf", [128, HW], F), "SQl": ("sbuf", [128, HW], F),
+    "Y": ("sbuf", [128, WI], F), "c18": ("sbuf", [128, WI], F),
+    "C4p": ("psum", [128, W], F), "C8p": ("psum", [128, W], F), "A": ("psum", [128, W], F), "ND": ("psum", [128, W], F),
+    "ABh": ("psum", [128, 128], F), "SQh": ("psum", [128, 128], F),
+    "E": ("sbuf", [128, 7, 12], F), "Kc": ("sbuf", [128, 7, 12], F), "G": ("sbuf", [128, 7, 12], F),
+    "P": ("sbuf", [128, 7, 8], F), "V": ("sbuf", [128, 7, 4], F),
+    "O": ("sbuf", [128, 8, 4], F), "NO": ("sbuf", [128, 8, 4], F), "NEG1": ("sbuf", [128, 8, 4], F),
+    "ABe": ("sbuf", [128, 8, 4], F), "SQe": ("sbuf", [128, 8, 4], F),
+    "R2": ("sbuf", [128, 8, 4], F), "FT": ("sbuf", [128, 4, 4], F),
+    "SC": ("sbuf", [128, 2], F), "SO": ("sbuf", [128, 2], F), "YE": ("sbuf", [128, 4], F),
+    "RL1": ("sbuf", [128, 12], F), "RL2": ("sbuf", [128, 4], F),
+}
+SEMAPHORES = ["lu", "lb", "le", "v", "a1", "a2", "h1", "h2", "ls", "st"]
+
+
+def _plan(T, topo):
+    cores = list(T.cores)
+    plan = []
+    for j, c in enumerate(cores):
+        others = [(j + k) % N for k in range(1, N)]
+        direct = [d for d in others if topo.may_write(c, cores[d])]
+        far = [d for d in others if not topo.may_write(c, cores[d])]
+        helpers = [x for x in range(NSIM)
+                   if far and x not in cores and topo.host(x) == topo.host(c) and topo.chip(x) == topo.chip(c)
+                   and topo.die(x) == topo.die(c) and all(topo.may_write(x, cores[d]) for d in far)]
+        helpers = helpers[:min(2, len(far))]
+        share = [far[i::len(helpers)] for i in range(len(helpers))]
+        plan.append((direct, helpers, share))
+    return plan
+
+
+def _mask(topo, src, dsts):
+    m = topo.mask(src, dsts[0])
+    for d in dsts[1:]:
+        m &= topo.mask(src, d)
+    return m
+
+
+def _engines(topo, src, dsts):
+    return bin(_mask(topo, src, dsts)).count("1")
+
+
+def _send(g, topo, src, src_ap, dsts, dst_aps, remote_sem, local_sem):
+    ids = []
+    for d in dsts:
+        rid, pid = topo.addr(d, src)
+        ids.append(DstId(rid=rid, pnc=pid))
+    g.remote_dma_fused([RemoteDMATransfer(dst_ids=ids, dma_engine_mask=_mask(topo, src, dsts), remote_sem=remote_sem,
+                                          srcs=[src_ap], dsts=list(dst_aps), alu_op=0)], local_sem=local_sem)
+    return _engines(topo, src, dsts)
+
+
+def _carrier(g, core, T, topo, j, share, n_in):
+    cores = list(T.cores)
+    dsts = [cores[d] for d in share]
+    left = 0
+    g.wait_ge(T.sem.h1, n_in)
+    left += _send(g, topo, core, T.RL1[:], dsts, [T.E[:, (j - d) % N, :] for d in share], T.sem.a1, T.sem.ls)
+    g.wait_ge(T.sem.h2, n_in)
+    left += _send(g, topo, core, T.RL2[:], dsts, [T.R2[:, (j - d) % N, :] for d in share], T.sem.a2, T.sem.ls)
+    g.wait_ge(T.sem.ls, left)
+
+
+def rank_program(g, core, T, topo):
+    plan = _plan(T, topo)
+    cores = list(T.cores)
+    rank = T.rank_of(core)
+    if rank is None:
+        for j in range(N):
+            direct, helpers, share = plan[j]
+            if core in helpers:
+                _carrier(g, core, T, topo, j, share[helpers.index(core)], _engines(topo, cores[j], helpers))
+        return
+
+    direct, helpers, share = plan[rank]
+    sem = T.sem
+    add, sub, mul, mx = AluOpType.add, AluOpType.subtract, AluOpType.mult, AluOpType.max
+    vq = g.vector
+    n = [0]
+
+    def chain():
+        if n[0]:
+            vq.wait_ge(sem.v, n[0])
+        n[0] += 1
+
+    def tt(out, a, b, op):
+        chain()
+        vq.tensor_tensor(out, a, b, op).then_inc(sem.v, 1)
+
+    def fill(ap, c):
+        chain()
+        vq.memset(ap, c).then_inc(sem.v, 1)
+
+    arrive = 0
+    for j in range(N):
+        if j == rank:
+            continue
+        dj, hj, sj = plan[j]
+        if rank in dj:
+            arrive += _engines(topo, cores[j], [cores[d] for d in dj])
+        else:
+            for h, s in zip(hj, sj):
+                if rank in s:
+                    arrive += _engines(topo, h, [cores[d] for d in s])
+
+    U, B, E, R2, A, ND, D = T.U, T.B, T.E, T.R2, T.A, T.ND, T.D
+    g.sync.dma_start(U[:], T.u[:]).then_inc(sem.lu, 16)
+    g.scalar.dma_start(B[:], T.b[:]).then_inc(sem.lb, 16)
+    g.sync.dma_start(E[:, 0, 0:4], T.u[:, W - 4:W]).then_inc(sem.le, 16)
+    g.scalar.dma_start(E[:, 0, 8:10], T.b[:, W - 2:W]).then_inc(sem.le, 16)
+    g.sync.dma_start(E[:, 0, 4:8], T.u[:, 0:4]).then_inc(sem.le, 16)
+    g.scalar.dma_start(E[:, 0, 10:12], T.b[:, 0:2]).then_inc(sem.le, 16)
+
+    fill(T.C4p[:, 0:WI], 4.0)
+    fill(T.C8p[:, 0:WI], 8.0)
+    fill(R2[:, 0, 2:4], 0.0)
+    a = A[:, 0:WI]
+    nd = ND[:, 0:WI]
+    vq.wait_ge(sem.lu, 16)
+    tt(a, U[:, 1:1 + WI], U[:, 3:3 + WI], add)
+    tt(a, a, U[:, 0:WI], add)
+    tt(a, a, U[:, 4:4 + WI], add)
+    tt(T.u8[:], U[:, 2:2 + WI], T.C8p[:, 0:WI], mul)
+    vq.wait_ge(sem.lb, 16)
+    tt(T.b4[:], B[:, 2:2 + WI], T.C4p[:, 0:WI], mul)
+    tt(a, a, T.b4[:], add)
+    tt(D[:], a, T.u8[:], sub)
+    tt(nd, T.u8[:], a, sub)
+    ABl, SQl, ABh, SQh = T.ABl, T.SQl, T.ABh[:, 0:HW], T.SQh[:, 0:HW]
+    tt(ABl[:], D[:, 0:HW], ND[:, 0:HW], mx)
+    tt(ABh, D[:, HW:WI], ND[:, HW:WI], mx)
+    tt(SQl[:], D[:, 0:HW], ND[:, 0:HW], mul)
+    tt(SQh, D[:, HW:WI], ND[:, HW:WI], mul)
+    tt(ABl[:], ABl[:], ABh, mx)
+    tt(SQl[:], SQl[:], SQh, add)
+    w = HW // 2
+    tt(ABl[:, 0:w], ABl[:, 0:w], ABl[:, w:2 * w], mx)
+    tt(SQl[:, 0:w], SQl[:, 0:w], SQl[:, w:2 * w], add)
+    tt(ABl[:, 0:31], ABl[:, 0:31], ABl[:, 32:63], mx)
+    tt(SQl[:, 0:31], SQl[:, 0:31], SQl[:, 32:63], add)
+    w = 16
+    while w >= 2:
+        tt(ABl[:, 0:w], ABl[:, 0:w], ABl[:, w:2 * w], mx)
+        tt(SQl[:, 0:w], SQl[:, 0:w], SQl[:, w:2 * w], add)
+        w //= 2
+    tt(R2[:, 0, 1:2], ABl[:, 0:1], ABl[:, 1:2], mx)
+    tt(R2[:, 0, 0:1], SQl[:, 0:1], SQl[:, 1:2], add)
+    n_msg2 = n[0]
+
+    fill(T.c18[:], 0.125)
+    tt(T.Y[:], a, T.c18[:], mul)
+    n_y = n[0]
+    Kc, G, P, V, O, NO = T.Kc, T.G, T.P, T.V, T.O, T.NO
+    fill(Kc[:], 4.0)
+    fill(Kc[:, :, 2:6], -8.0)
+    fill(T.NEG1[:], -1.0)
+    fill(O[:, 6:8, :], 0.0)
+    fill(T.SC[:, 0:1], -1.0 / (64.0 * N * W))
+    fill(T.SC[:, 1:2], 0.125)
+    vq.wait_ge(sem.le, 64)
+    chain()
+    vq.tensor_copy(E[:, 6, :], E[:, 0, :]).then_inc(sem.v, 1)
+    vq.wait_ge(sem.a1, arrive)
+    tt(G[:], E[:], Kc[:], mul)
+    tt(V[:], G[:, :, 2:6], G[:, :, 8:12], add)
+    tt(P[:, :, 0:7], E[:, :, 0:7], E[:, :, 1:8], add)
+    tt(V[:, :, 0:2], V[:, :, 0:2], P[:, :, 0:2], add)
+    tt(V[:, :, 2:4], V[:, :, 2:4], P[:, :, 5:7], add)
+    tt(V[:, :, 0:1], V[:, :, 0:1], E[:, :, 3:4], add)
+    tt(V[:, :, 3:4], V[:, :, 3:4], E[:, :, 4:5], add)
+    tt(O[:, 0:6, 0:1], V[:, 0:6, 0:1], E[:, 1:7, 4:5], add)
+    tt(O[:, 0:6, 1:2], V[:, 0:6, 1:2], P[:, 1:7, 4:5], add)
+    tt(O[:, 0:6, 2:3], V[:, 1:7, 2:3], P[:, 0:6, 2:3], add)
+    tt(O[:, 0:6, 3:4], V[:, 1:7, 3:4], E[:, 0:6, 3:4], add)
+    tt(T.YE[:, 0:2], O[:, 0, 0:2], T.c18[:, 0:2], mul)
+    tt(T.YE[:, 2:4], O[:, 5, 2:4], T.c18[:, 0:2], mul)
+    tt(T.YE[:], T.YE[:], E[:, 0, 2:6], add)
+    n_ye = n[0]
+    ABe, SQe = T.ABe, T.SQe
+    tt(NO[:], O[:], T.NEG1[:], mul)
+    tt(ABe[:], O[:], NO[:], mx)
+    tt(SQe[:], O[:], NO[:], mul)
+    for w in (4, 2, 1):
+        tt(ABe[:, 0:w, :], ABe[:, 0:w, :], ABe[:, w:2 * w, :], mx)
+        tt(SQe[:, 0:w, :], SQe[:, 0:w, :], SQe[:, w:2 * w, :], add)
+    tt(R2[:, 6:8, 1], ABe[:, 0, 0:2], ABe[:, 0, 2:4], mx)
+    tt(R2[:, 6:8, 0], SQe[:, 0, 0:2], SQe[:, 0, 2:4], add)
+
+    FT = T.FT
+    vq.wait_ge(sem.a2, arrive)
+    tt(FT[:, 0:4, 0:1], R2[:, 0:4, 0:1], R2[:, 4:8, 0:1], add)
+    tt(FT[:, 0:4, 1:2], R2[:, 0:4, 1:2], R2[:, 4:8, 1:2], mx)
+    for w in (2, 1):
+        tt(FT[:, 0:w, 0:1], FT[:, 0:w, 0:1], FT[:, w:2 * w, 0:1], add)
+        tt(FT[:, 0:w, 1:2], FT[:, 0:w, 1:2], FT[:, w:2 * w, 1:2], mx)
+    tt(T.SO[:], FT[:, 0, 0:2], T.SC[:], mul)
+    n_s = n[0]
+
+    g.sync.wait_ge(sem.v, n_y)
+    g.sync.dma_start(T.y[:, 2:2 + WI], T.Y[:]).then_inc(sem.st, 16)
+    g.scalar.wait_ge(sem.v, n_ye)
+    g.scalar.dma_start(T.y[:, W - 2:W], T.YE[:, 0:2]).then_inc(sem.st, 16)
+    g.scalar.dma_start(T.y[:, 0:2], T.YE[:, 2:4]).then_inc(sem.st, 16)
+    g.sync.wait_ge(sem.v, n_s)
+    g.sync.dma_start(T.s[:], T.SO[:]).then_inc(sem.st, 16)
+
+    left = 0
+    for ready, count, src, relay, hsem, land, asem in (
+            (sem.le, 64, E[:, 0, :], T.RL1, sem.h1, E, sem.a1),
+            (sem.v, n_msg2, R2[:, 0, :], T.RL2, sem.h2, R2, sem.a2)):
+        g.wait_ge(ready, count)
+        if helpers:
+            left += _send(g, topo, core, src, helpers, [relay[:] for h in helpers], hsem, sem.ls)
+        if direct:
+            left += _send(g, topo, core, src, [cores[d] for d in direct],
+                          [land[:, (rank - d) % N, :] for d in direct], asem, sem.ls)
+    g.wait_ge(sem.ls, left)
+    g.wait_ge(sem.st, 64)

@@ -6,6 +6,7 @@ W = 256
 WI = W - 4
 HW = WI // 2
 NSIM = 256
+ES = 20
 
 F = "float32"
 SCRATCH = {
@@ -15,15 +16,14 @@ SCRATCH = {
     "Y": ("sbuf", [128, WI], F), "c18": ("sbuf", [128, WI], F),
     "C4p": ("psum", [128, W], F), "C8p": ("psum", [128, W], F), "A": ("psum", [128, W], F), "ND": ("psum", [128, W], F),
     "ABh": ("psum", [128, 128], F), "SQh": ("psum", [128, 128], F),
-    "E": ("sbuf", [128, 7, 12], F), "Kc": ("sbuf", [128, 7, 12], F), "G": ("sbuf", [128, 7, 12], F),
-    "P": ("sbuf", [128, 7, 8], F), "V": ("sbuf", [128, 7, 4], F),
-    "O": ("sbuf", [128, 8, 4], F), "NO": ("sbuf", [128, 8, 4], F), "NEG1": ("sbuf", [128, 8, 4], F),
-    "ABe": ("sbuf", [128, 8, 4], F), "SQe": ("sbuf", [128, 8, 4], F),
-    "R2": ("sbuf", [128, 8, 4], F), "FT": ("sbuf", [128, 4, 4], F),
+    "E": ("sbuf", [128, 7, ES], F), "Kc": ("sbuf", [128, 7, ES], F), "G": ("sbuf", [128, 7, ES], F),
+    "P": ("sbuf", [128, 7, 12], F), "Q": ("sbuf", [128, 7, 8], F), "H": ("sbuf", [128, 7, 8], F),
+    "O": ("sbuf", [128, 6, 4], F), "NO": ("sbuf", [128, 6, 4], F), "NEG1": ("sbuf", [128, 6, 4], F),
+    "Z": ("sbuf", [128, 8, 4, 2], F),
     "SC": ("sbuf", [128, 2], F), "SO": ("sbuf", [128, 2], F), "YE": ("sbuf", [128, 4], F),
-    "RL1": ("sbuf", [128, 12], F), "RL2": ("sbuf", [128, 4], F),
+    "RL1": ("sbuf", [128, ES], F), "RL2": ("sbuf", [128, 2], F),
 }
-SEMAPHORES = ["lu", "lb", "le", "v", "a1", "a2", "h1", "h2", "ls", "st"]
+SEMAPHORES = ["lu", "lb", "le", "l6", "v", "a1", "a2", "h1", "h2", "ls", "st"]
 
 
 def _plan(T, topo):
@@ -63,14 +63,23 @@ def _send(g, topo, src, src_ap, dsts, dst_aps, remote_sem, local_sem):
     return _engines(topo, src, dsts)
 
 
+def _eslot(T, j, d):
+    return T.E[:, (j - d) % N, :]
+
+
+def _zslot(T, j, d):
+    e = 25 + (j - d) % N
+    return T.Z[:, e // 4, e % 4, :]
+
+
 def _carrier(g, core, T, topo, j, share, n_in):
     cores = list(T.cores)
     dsts = [cores[d] for d in share]
     left = 0
     g.wait_ge(T.sem.h1, n_in)
-    left += _send(g, topo, core, T.RL1[:], dsts, [T.E[:, (j - d) % N, :] for d in share], T.sem.a1, T.sem.ls)
+    left += _send(g, topo, core, T.RL1[:], dsts, [_eslot(T, j, d) for d in share], T.sem.a1, T.sem.ls)
     g.wait_ge(T.sem.h2, n_in)
-    left += _send(g, topo, core, T.RL2[:], dsts, [T.R2[:, (j - d) % N, :] for d in share], T.sem.a2, T.sem.ls)
+    left += _send(g, topo, core, T.RL2[:], dsts, [_zslot(T, j, d) for d in share], T.sem.a2, T.sem.ls)
     g.wait_ge(T.sem.ls, left)
 
 
@@ -116,17 +125,32 @@ def rank_program(g, core, T, topo):
                 if rank in s:
                     arrive += _engines(topo, h, [cores[d] for d in s])
 
-    U, B, E, R2, A, ND, D = T.U, T.B, T.E, T.R2, T.A, T.ND, T.D
+    U, B, E, Z, A, ND, D = T.U, T.B, T.E, T.Z, T.A, T.ND, T.D
+    Kc, G, P, Q, H, O, NO = T.Kc, T.G, T.P, T.Q, T.H, T.O, T.NO
+
+    fill(E[:, 0, :], 0.0)
+    fill(T.C8p[:, 0:WI], 8.0)
+    fill(T.C4p[:, 0:WI], 4.0)
+    fill(Z[:, 6, 1, :], 0.0)
+    fill(T.c18[:], 0.125)
+    fill(Kc[:, :, 2:12], -8.0)
+    fill(Kc[:, :, 12:20], 4.0)
+    fill(T.NEG1[:], -1.0)
+    fill(T.SC[:, 0:1], -1.0 / (64.0 * N * W))
+    fill(T.SC[:, 1:2], 0.125)
+
     g.sync.dma_start(U[:], T.u[:]).then_inc(sem.lu, 16)
     g.scalar.dma_start(B[:], T.b[:]).then_inc(sem.lb, 16)
+    g.sync.wait_ge(sem.v, 1)
+    g.scalar.wait_ge(sem.v, 1)
     g.sync.dma_start(E[:, 0, 0:4], T.u[:, W - 4:W]).then_inc(sem.le, 16)
-    g.scalar.dma_start(E[:, 0, 8:10], T.b[:, W - 2:W]).then_inc(sem.le, 16)
-    g.sync.dma_start(E[:, 0, 4:8], T.u[:, 0:4]).then_inc(sem.le, 16)
-    g.scalar.dma_start(E[:, 0, 10:12], T.b[:, 0:2]).then_inc(sem.le, 16)
+    g.scalar.dma_start(E[:, 0, 12:14], T.b[:, W - 2:W]).then_inc(sem.le, 16)
+    g.sync.dma_start(E[:, 0, 8:12], T.u[:, 0:4]).then_inc(sem.le, 16)
+    g.scalar.dma_start(E[:, 0, 18:20], T.b[:, 0:2]).then_inc(sem.le, 16)
+    g.scalar.dma_start(Z[:, 7, 3, :], E[:, 0, 4:6]).then_inc(sem.l6, 16)
+    g.sync.wait_ge(sem.le, 64)
+    g.sync.dma_start(E[:, 6, :], E[:, 0, :]).then_inc(sem.l6, 16)
 
-    fill(T.C4p[:, 0:WI], 4.0)
-    fill(T.C8p[:, 0:WI], 8.0)
-    fill(R2[:, 0, 2:4], 0.0)
     a = A[:, 0:WI]
     nd = ND[:, 0:WI]
     vq.wait_ge(sem.lu, 16)
@@ -156,57 +180,37 @@ def rank_program(g, core, T, topo):
         tt(ABl[:, 0:w], ABl[:, 0:w], ABl[:, w:2 * w], mx)
         tt(SQl[:, 0:w], SQl[:, 0:w], SQl[:, w:2 * w], add)
         w //= 2
-    tt(R2[:, 0, 1:2], ABl[:, 0:1], ABl[:, 1:2], mx)
-    tt(R2[:, 0, 0:1], SQl[:, 0:1], SQl[:, 1:2], add)
+    tt(Z[:, 6, 0, 1:2], ABl[:, 0:1], ABl[:, 1:2], mx)
+    tt(Z[:, 6, 0, 0:1], SQl[:, 0:1], SQl[:, 1:2], add)
     n_msg2 = n[0]
-
-    fill(T.c18[:], 0.125)
     tt(T.Y[:], a, T.c18[:], mul)
     n_y = n[0]
-    Kc, G, P, V, O, NO = T.Kc, T.G, T.P, T.V, T.O, T.NO
-    fill(Kc[:], 4.0)
-    fill(Kc[:, :, 2:6], -8.0)
-    fill(T.NEG1[:], -1.0)
-    fill(O[:, 6:8, :], 0.0)
-    fill(T.SC[:, 0:1], -1.0 / (64.0 * N * W))
-    fill(T.SC[:, 1:2], 0.125)
-    vq.wait_ge(sem.le, 64)
-    chain()
-    vq.tensor_copy(E[:, 6, :], E[:, 0, :]).then_inc(sem.v, 1)
+
+    vq.wait_ge(sem.l6, 32)
     vq.wait_ge(sem.a1, arrive)
-    tt(G[:], E[:], Kc[:], mul)
-    tt(V[:], G[:, :, 2:6], G[:, :, 8:12], add)
-    tt(P[:, :, 0:7], E[:, :, 0:7], E[:, :, 1:8], add)
-    tt(V[:, :, 0:2], V[:, :, 0:2], P[:, :, 0:2], add)
-    tt(V[:, :, 2:4], V[:, :, 2:4], P[:, :, 5:7], add)
-    tt(V[:, :, 0:1], V[:, :, 0:1], E[:, :, 3:4], add)
-    tt(V[:, :, 3:4], V[:, :, 3:4], E[:, :, 4:5], add)
-    tt(O[:, 0:6, 0:1], V[:, 0:6, 0:1], E[:, 1:7, 4:5], add)
-    tt(O[:, 0:6, 1:2], V[:, 0:6, 1:2], P[:, 1:7, 4:5], add)
-    tt(O[:, 0:6, 2:3], V[:, 1:7, 2:3], P[:, 0:6, 2:3], add)
-    tt(O[:, 0:6, 3:4], V[:, 1:7, 3:4], E[:, 0:6, 3:4], add)
+    tt(G[:, :, 2:20], E[:, :, 2:20], Kc[:, :, 2:20], mul)
+    tt(P[:, :, 0:11], E[:, :, 0:11], E[:, :, 1:12], add)
+    tt(Q[:], P[:, :, 0:8], P[:, :, 3:11], add)
+    tt(H[:], G[:, :, 2:10], G[:, :, 12:20], add)
+    tt(Q[:], Q[:], H[:], add)
+    tt(O[:], Q[:, 0:6, 0:4], Q[:, 1:7, 4:8], add)
     tt(T.YE[:, 0:2], O[:, 0, 0:2], T.c18[:, 0:2], mul)
     tt(T.YE[:, 2:4], O[:, 5, 2:4], T.c18[:, 0:2], mul)
-    tt(T.YE[:], T.YE[:], E[:, 0, 2:6], add)
+    tt(T.YE[:, 0:2], T.YE[:, 0:2], U[:, W - 2:W], add)
+    tt(T.YE[:, 2:4], T.YE[:, 2:4], U[:, 0:2], add)
     n_ye = n[0]
-    ABe, SQe = T.ABe, T.SQe
     tt(NO[:], O[:], T.NEG1[:], mul)
-    tt(ABe[:], O[:], NO[:], mx)
-    tt(SQe[:], O[:], NO[:], mul)
-    for w in (4, 2, 1):
-        tt(ABe[:, 0:w, :], ABe[:, 0:w, :], ABe[:, w:2 * w, :], mx)
-        tt(SQe[:, 0:w, :], SQe[:, 0:w, :], SQe[:, w:2 * w, :], add)
-    tt(R2[:, 6:8, 1], ABe[:, 0, 0:2], ABe[:, 0, 2:4], mx)
-    tt(R2[:, 6:8, 0], SQe[:, 0, 0:2], SQe[:, 0, 2:4], add)
+    tt(Z[:, 0:6, :, 1], O[:], NO[:], mx)
+    tt(Z[:, 0:6, :, 0], O[:], NO[:], mul)
 
-    FT = T.FT
     vq.wait_ge(sem.a2, arrive)
-    tt(FT[:, 0:4, 0:1], R2[:, 0:4, 0:1], R2[:, 4:8, 0:1], add)
-    tt(FT[:, 0:4, 1:2], R2[:, 0:4, 1:2], R2[:, 4:8, 1:2], mx)
+    for w in (4, 2, 1):
+        tt(Z[:, 0:w, :, 0:1], Z[:, 0:w, :, 0:1], Z[:, w:2 * w, :, 0:1], add)
+        tt(Z[:, 0:w, :, 1:2], Z[:, 0:w, :, 1:2], Z[:, w:2 * w, :, 1:2], mx)
     for w in (2, 1):
-        tt(FT[:, 0:w, 0:1], FT[:, 0:w, 0:1], FT[:, w:2 * w, 0:1], add)
-        tt(FT[:, 0:w, 1:2], FT[:, 0:w, 1:2], FT[:, w:2 * w, 1:2], mx)
-    tt(T.SO[:], FT[:, 0, 0:2], T.SC[:], mul)
+        tt(Z[:, 0, 0:w, 0:1], Z[:, 0, 0:w, 0:1], Z[:, 0, w:2 * w, 0:1], add)
+        tt(Z[:, 0, 0:w, 1:2], Z[:, 0, 0:w, 1:2], Z[:, 0, w:2 * w, 1:2], mx)
+    tt(T.SO[:], Z[:, 0, 0, :], T.SC[:], mul)
     n_s = n[0]
 
     g.sync.wait_ge(sem.v, n_y)
@@ -218,14 +222,14 @@ def rank_program(g, core, T, topo):
     g.sync.dma_start(T.s[:], T.SO[:]).then_inc(sem.st, 16)
 
     left = 0
-    for ready, count, src, relay, hsem, land, asem in (
-            (sem.le, 64, E[:, 0, :], T.RL1, sem.h1, E, sem.a1),
-            (sem.v, n_msg2, R2[:, 0, :], T.RL2, sem.h2, R2, sem.a2)):
+    for ready, count, src, relay, hsem, slot, asem in (
+            (sem.le, 64, E[:, 0, :], T.RL1, sem.h1, _eslot, sem.a1),
+            (sem.v, n_msg2, Z[:, 6, 0, :], T.RL2, sem.h2, _zslot, sem.a2)):
         g.wait_ge(ready, count)
         if helpers:
             left += _send(g, topo, core, src, helpers, [relay[:] for h in helpers], hsem, sem.ls)
         if direct:
             left += _send(g, topo, core, src, [cores[d] for d in direct],
-                          [land[:, (rank - d) % N, :] for d in direct], asem, sem.ls)
+                          [slot(T, rank, d) for d in direct], asem, sem.ls)
     g.wait_ge(sem.ls, left)
     g.wait_ge(sem.st, 64)

@@ -3,27 +3,30 @@ from concourse.mybir import AluOpType
 
 N = 6
 W = 256
+WP = W + 8
+WD = W + 4
 WI = W - 4
 HW = WI // 2
 NSIM = 256
-ES = 20
 
 F = "float32"
 SCRATCH = {
-    "U": ("sbuf", [128, W], F), "B": ("sbuf", [128, W], F),
-    "b4": ("sbuf", [128, WI], F), "u8": ("sbuf", [128, WI], F), "D": ("sbuf", [128, WI], F),
-    "ABl": ("sbuf", [128, HW], F), "SQl": ("sbuf", [128, HW], F),
-    "Y": ("sbuf", [128, WI], F), "c18": ("sbuf", [128, WI], F),
-    "C4p": ("psum", [128, W], F), "C8p": ("psum", [128, W], F), "A": ("psum", [128, W], F), "ND": ("psum", [128, W], F),
-    "ABh": ("psum", [128, 128], F), "SQh": ("psum", [128, 128], F),
-    "E": ("sbuf", [128, 7, ES], F), "Kc": ("sbuf", [128, 7, ES], F), "G": ("sbuf", [128, 7, ES], F),
-    "P": ("sbuf", [128, 7, 12], F), "Q": ("sbuf", [128, 7, 8], F), "H": ("sbuf", [128, 7, 8], F),
-    "O": ("sbuf", [128, 6, 4], F), "NO": ("sbuf", [128, 6, 4], F), "NEG1": ("sbuf", [128, 6, 4], F),
-    "Z": ("sbuf", [128, 8, 4, 2], F),
-    "SC": ("sbuf", [128, 2], F), "SO": ("sbuf", [128, 2], F), "YE": ("sbuf", [128, 4], F),
-    "RL1": ("sbuf", [128, ES], F), "RL2": ("sbuf", [128, 2], F),
+    "UB": ("sbuf", [128, 2, WP], F), "Pm": ("sbuf", [128, WP], F),
+    "b4": ("sbuf", [128, WD], F), "u8": ("sbuf", [128, WD], F), "D": ("sbuf", [128, WD], F),
+    "ABl": ("sbuf", [128, HW], F), "SQ": ("sbuf", [128, WI], F),
+    "Y": ("sbuf", [128, W], F), "c18": ("sbuf", [128, W], F),
+    "C4p": ("psum", [128, 512], F), "C8p": ("psum", [128, 512], F), "A": ("psum", [128, 512], F),
+    "ND": ("psum", [128, 512], F), "ABh": ("psum", [128, 512], F), "TP": ("psum", [128, 512], F), "SP": ("psum", [128, 512], F),
+    "Zi": ("sbuf", [128, 129], F), "IDd": ("dram", [128 * 129], F), "I": ("sbuf", [128, 128], F),
+    "Ts": ("sbuf", [128, 128], F), "one": ("sbuf", [128, 1], F),
+    "RR": ("sbuf", [128, 6, 4], F), "LL": ("sbuf", [128, 6, 4], F),
+    "O": ("sbuf", [128, 8, 4], F), "NO": ("sbuf", [128, 8, 4], F), "NEG1": ("sbuf", [128, 8, 4], F),
+    "ABe": ("sbuf", [128, 8, 4], F), "SQe": ("sbuf", [128, 8, 4], F),
+    "R2": ("sbuf", [128, 8, 4], F), "FT": ("sbuf", [128, 4, 4], F),
+    "SC": ("sbuf", [128, 2], F), "SO": ("sbuf", [128, 2], F),
+    "RL1": ("sbuf", [128, 2, 4], F), "RL2": ("sbuf", [128, 4], F),
 }
-SEMAPHORES = ["lu", "lb", "le", "l6", "v", "a1", "a2", "h1", "h2", "ls", "st"]
+SEMAPHORES = ["lu", "lb", "l6", "i1", "i2", "pe", "v", "a1", "a2", "h1", "h2", "ls", "st"]
 
 
 def _plan(T, topo):
@@ -53,23 +56,28 @@ def _engines(topo, src, dsts):
     return bin(_mask(topo, src, dsts)).count("1")
 
 
-def _send(g, topo, src, src_ap, dsts, dst_aps, remote_sem, local_sem):
+def _send(g, topo, src, parts, dsts, remote_sem, local_sem):
     ids = []
     for d in dsts:
         rid, pid = topo.addr(d, src)
         ids.append(DstId(rid=rid, pnc=pid))
-    g.remote_dma_fused([RemoteDMATransfer(dst_ids=ids, dma_engine_mask=_mask(topo, src, dsts), remote_sem=remote_sem,
-                                          srcs=[src_ap], dsts=list(dst_aps), alu_op=0)], local_sem=local_sem)
-    return _engines(topo, src, dsts)
+    m = _mask(topo, src, dsts)
+    bits = [1 << i for i in range(m.bit_length()) if (m >> i) & 1]
+    k = len(bits) // len(parts)
+    trs = []
+    for i, (s_ap, d_aps) in enumerate(parts):
+        trs.append(RemoteDMATransfer(dst_ids=ids, dma_engine_mask=sum(bits[i * k:(i + 1) * k]), remote_sem=remote_sem,
+                                     srcs=[s_ap], dsts=list(d_aps), alu_op=0))
+    g.remote_dma_fused(trs, local_sem=local_sem)
+    return k * len(parts)
 
 
-def _eslot(T, j, d):
-    return T.E[:, (j - d) % N, :]
+def _m1(T, right, left, j, ds):
+    return [(right, [T.RR[:, (j - d) % N, :] for d in ds]), (left, [T.LL[:, (j - d) % N - 1, :] for d in ds])]
 
 
-def _zslot(T, j, d):
-    e = 25 + (j - d) % N
-    return T.Z[:, e // 4, e % 4, :]
+def _m2(T, src, j, ds):
+    return [(src, [T.R2[:, (j - d) % N, :] for d in ds])]
 
 
 def _carrier(g, core, T, topo, j, share, n_in):
@@ -77,9 +85,9 @@ def _carrier(g, core, T, topo, j, share, n_in):
     dsts = [cores[d] for d in share]
     left = 0
     g.wait_ge(T.sem.h1, n_in)
-    left += _send(g, topo, core, T.RL1[:], dsts, [_eslot(T, j, d) for d in share], T.sem.a1, T.sem.ls)
+    left += _send(g, topo, core, _m1(T, T.RL1[:, 0, :], T.RL1[:, 1, :], j, share), dsts, T.sem.a1, T.sem.ls)
     g.wait_ge(T.sem.h2, n_in)
-    left += _send(g, topo, core, T.RL2[:], dsts, [_zslot(T, j, d) for d in share], T.sem.a2, T.sem.ls)
+    left += _send(g, topo, core, _m2(T, T.RL2[:], j, share), dsts, T.sem.a2, T.sem.ls)
     g.wait_ge(T.sem.ls, left)
 
 
@@ -113,6 +121,10 @@ def rank_program(g, core, T, topo):
         chain()
         vq.memset(ap, c).then_inc(sem.v, 1)
 
+    def copy(out, in_):
+        chain()
+        vq.tensor_copy(out, in_).then_inc(sem.v, 1)
+
     arrive = 0
     for j in range(N):
         if j == rank:
@@ -125,111 +137,118 @@ def rank_program(g, core, T, topo):
                 if rank in s:
                     arrive += _engines(topo, h, [cores[d] for d in s])
 
-    U, B, E, Z, A, ND, D = T.U, T.B, T.E, T.Z, T.A, T.ND, T.D
-    Kc, G, P, Q, H, O, NO = T.Kc, T.G, T.P, T.Q, T.H, T.O, T.NO
+    UB, R2, A, ND, D, O, NO = T.UB, T.R2, T.A, T.ND, T.D, T.O, T.NO
+    U, B = UB[:, 0, :], UB[:, 1, :]
 
-    fill(E[:, 0, :], 0.0)
-    fill(T.C8p[:, 0:WI], 8.0)
-    fill(T.C4p[:, 0:WI], 4.0)
-    fill(Z[:, 6, 1, :], 0.0)
-    fill(T.c18[:], 0.125)
-    fill(Kc[:, :, 2:12], -8.0)
-    fill(Kc[:, :, 12:20], 4.0)
+    fill(T.Zi[:], 0.0)
+    fill(T.Zi[:, 0:1], 1.0)
+    n_zi = n[0]
+    fill(UB[:, :, 0:4], 0.0)
+    fill(UB[:, :, WP - 4:WP], 0.0)
+    fill(T.C8p[:, 0:WD], 8.0)
+    fill(T.C4p[:, 0:WD], 4.0)
+    fill(T.one[:], 1.0)
+    fill(R2[:, 0, 2:4], 0.0)
+    fill(O[:, 6:8, :], 0.0)
     fill(T.NEG1[:], -1.0)
+    fill(T.c18[:], 0.125)
     fill(T.SC[:, 0:1], -1.0 / (64.0 * N * W))
     fill(T.SC[:, 1:2], 0.125)
 
-    g.sync.dma_start(U[:], T.u[:]).then_inc(sem.lu, 16)
-    g.scalar.dma_start(B[:], T.b[:]).then_inc(sem.lb, 16)
-    g.sync.wait_ge(sem.v, 1)
-    g.scalar.wait_ge(sem.v, 1)
-    g.sync.dma_start(E[:, 0, 0:4], T.u[:, W - 4:W]).then_inc(sem.le, 16)
-    g.scalar.dma_start(E[:, 0, 12:14], T.b[:, W - 2:W]).then_inc(sem.le, 16)
-    g.sync.dma_start(E[:, 0, 8:12], T.u[:, 0:4]).then_inc(sem.le, 16)
-    g.scalar.dma_start(E[:, 0, 18:20], T.b[:, 0:2]).then_inc(sem.le, 16)
-    g.scalar.dma_start(Z[:, 7, 3, :], E[:, 0, 4:6]).then_inc(sem.l6, 16)
-    g.sync.wait_ge(sem.le, 64)
-    g.sync.dma_start(E[:, 6, :], E[:, 0, :]).then_inc(sem.l6, 16)
+    g.sync.dma_start(UB[0:64, 0, 4:4 + W], T.u[0:64, :]).then_inc(sem.lu, 16)
+    g.scalar.dma_start(UB[64:128, 0, 4:4 + W], T.u[64:128, :]).then_inc(sem.lu, 16)
+    g.sync.dma_start(UB[0:64, 1, 4:4 + W], T.b[0:64, :]).then_inc(sem.lb, 16)
+    g.scalar.dma_start(UB[64:128, 1, 4:4 + W], T.b[64:128, :]).then_inc(sem.lb, 16)
+    g.sync.wait_ge(sem.v, n_zi)
+    g.sync.dma_start(T.IDd[:], T.Zi[:]).then_inc(sem.i1, 16)
+    g.sync.wait_ge(sem.i1, 16)
+    g.sync.dma_start(T.I[:], T.IDd[0:128 * 128]).then_inc(sem.i2, 16)
 
-    a = A[:, 0:WI]
-    nd = ND[:, 0:WI]
-    vq.wait_ge(sem.lu, 16)
-    tt(a, U[:, 1:1 + WI], U[:, 3:3 + WI], add)
-    tt(a, a, U[:, 0:WI], add)
-    tt(a, a, U[:, 4:4 + WI], add)
-    tt(T.u8[:], U[:, 2:2 + WI], T.C8p[:, 0:WI], mul)
-    vq.wait_ge(sem.lb, 16)
-    tt(T.b4[:], B[:, 2:2 + WI], T.C4p[:, 0:WI], mul)
+    a = A[:, 0:WD]
+    vq.wait_ge(sem.lu, 32)
+    tt(T.Pm[:, 0:WP - 1], UB[:, 0, 0:WP - 1], UB[:, 0, 1:WP], add)
+    tt(a, T.Pm[:, 0:WD], T.Pm[:, 3:3 + WD], add)
+    tt(T.u8[:], UB[:, 0, 2:2 + WD], T.C8p[:, 0:WD], mul)
+    vq.wait_ge(sem.lb, 32)
+    tt(T.b4[:], UB[:, 1, 2:2 + WD], T.C4p[:, 0:WD], mul)
     tt(a, a, T.b4[:], add)
     tt(D[:], a, T.u8[:], sub)
-    tt(nd, T.u8[:], a, sub)
-    ABl, SQl, ABh, SQh = T.ABl, T.SQl, T.ABh[:, 0:HW], T.SQh[:, 0:HW]
-    tt(ABl[:], D[:, 0:HW], ND[:, 0:HW], mx)
-    tt(ABh, D[:, HW:WI], ND[:, HW:WI], mx)
-    tt(SQl[:], D[:, 0:HW], ND[:, 0:HW], mul)
-    tt(SQh, D[:, HW:WI], ND[:, HW:WI], mul)
+    n_d = n[0]
+    tt(ND[:, 0:WI], T.u8[:, 4:4 + WI], A[:, 4:4 + WI], sub)
+    tt(T.SQ[:], D[:, 4:4 + WI], ND[:, 0:WI], mul)
+    n_sq = n[0]
+    ABl, ABh = T.ABl, T.ABh[:, 0:HW]
+    tt(ABl[:], D[:, 4:4 + HW], ND[:, 0:HW], mx)
+    tt(ABh, D[:, 4 + HW:4 + WI], ND[:, HW:WI], mx)
     tt(ABl[:], ABl[:], ABh, mx)
-    tt(SQl[:], SQl[:], SQh, add)
-    w = HW // 2
-    tt(ABl[:, 0:w], ABl[:, 0:w], ABl[:, w:2 * w], mx)
-    tt(SQl[:, 0:w], SQl[:, 0:w], SQl[:, w:2 * w], add)
+    tt(ABl[:, 0:63], ABl[:, 0:63], ABl[:, 63:126], mx)
     tt(ABl[:, 0:31], ABl[:, 0:31], ABl[:, 32:63], mx)
-    tt(SQl[:, 0:31], SQl[:, 0:31], SQl[:, 32:63], add)
-    w = 16
-    while w >= 2:
+    tt(ABl[:, 0:16], ABl[:, 0:16], ABl[:, 16:32], mx)
+    vq.wait_ge(sem.pe, 1)
+    copy(T.Ts[0:HW, :], T.TP[0:HW, 0:128])
+    n_ts = n[0]
+    for w in (8, 4, 2):
         tt(ABl[:, 0:w], ABl[:, 0:w], ABl[:, w:2 * w], mx)
-        tt(SQl[:, 0:w], SQl[:, 0:w], SQl[:, w:2 * w], add)
-        w //= 2
-    tt(Z[:, 6, 0, 1:2], ABl[:, 0:1], ABl[:, 1:2], mx)
-    tt(Z[:, 6, 0, 0:1], SQl[:, 0:1], SQl[:, 1:2], add)
+    tt(R2[:, 0, 1:2], ABl[:, 0:1], ABl[:, 1:2], mx)
+    vq.wait_ge(sem.pe, 2)
+    copy(R2[:, 0, 0:1], T.SP[:, 0:1])
     n_msg2 = n[0]
-    tt(T.Y[:], a, T.c18[:], mul)
-    n_y = n[0]
+
+    tq = g.tensor
+    tq.wait_ge(sem.i2, 16)
+    tq.wait_ge(sem.v, n_sq)
+    tq.matmul(T.TP[0:HW, 0:128], T.SQ[:, 0:HW], T.I[:], True, False)
+    tq.matmul(T.TP[0:HW, 0:128], T.SQ[:, HW:WI], T.I[:], False, True).then_inc(sem.pe, 1)
+    tq.wait_ge(sem.v, n_ts)
+    tq.matmul(T.SP[:, 0:1], T.Ts[0:HW, :], T.one[0:HW, :], True, True).then_inc(sem.pe, 1)
 
     vq.wait_ge(sem.l6, 32)
     vq.wait_ge(sem.a1, arrive)
-    tt(G[:, :, 2:20], E[:, :, 2:20], Kc[:, :, 2:20], mul)
-    tt(P[:, :, 0:11], E[:, :, 0:11], E[:, :, 1:12], add)
-    tt(Q[:], P[:, :, 0:8], P[:, :, 3:11], add)
-    tt(H[:], G[:, :, 2:10], G[:, :, 12:20], add)
-    tt(Q[:], Q[:], H[:], add)
-    tt(O[:], Q[:, 0:6, 0:4], Q[:, 1:7, 4:8], add)
-    tt(T.YE[:, 0:2], O[:, 0, 0:2], T.c18[:, 0:2], mul)
-    tt(T.YE[:, 2:4], O[:, 5, 2:4], T.c18[:, 0:2], mul)
-    tt(T.YE[:, 0:2], T.YE[:, 0:2], U[:, W - 2:W], add)
-    tt(T.YE[:, 2:4], T.YE[:, 2:4], U[:, 0:2], add)
-    n_ye = n[0]
+    tt(O[:, 0:6, :], T.RR[:], T.LL[:], add)
+    tt(A[:, 2:4], O[:, 5, 2:4], T.u8[:, 2:4], add)
+    tt(A[:, W:W + 2], O[:, 0, 0:2], T.u8[:, W:W + 2], add)
+    tt(T.Y[:], A[:, 2:2 + W], T.c18[:], mul)
+    n_y = n[0]
+    ABe, SQe = T.ABe, T.SQe
     tt(NO[:], O[:], T.NEG1[:], mul)
-    tt(Z[:, 0:6, :, 1], O[:], NO[:], mx)
-    tt(Z[:, 0:6, :, 0], O[:], NO[:], mul)
-
-    vq.wait_ge(sem.a2, arrive)
+    tt(ABe[:], O[:], NO[:], mx)
+    tt(SQe[:], O[:], NO[:], mul)
     for w in (4, 2, 1):
-        tt(Z[:, 0:w, :, 0:1], Z[:, 0:w, :, 0:1], Z[:, w:2 * w, :, 0:1], add)
-        tt(Z[:, 0:w, :, 1:2], Z[:, 0:w, :, 1:2], Z[:, w:2 * w, :, 1:2], mx)
+        tt(ABe[:, 0:w, :], ABe[:, 0:w, :], ABe[:, w:2 * w, :], mx)
+        tt(SQe[:, 0:w, :], SQe[:, 0:w, :], SQe[:, w:2 * w, :], add)
+    tt(R2[:, 6:8, 1], ABe[:, 0, 0:2], ABe[:, 0, 2:4], mx)
+    tt(R2[:, 6:8, 0], SQe[:, 0, 0:2], SQe[:, 0, 2:4], add)
+
+    FT = T.FT
+    vq.wait_ge(sem.a2, arrive)
+    tt(FT[:, 0:4, 0:1], R2[:, 0:4, 0:1], R2[:, 4:8, 0:1], add)
+    tt(FT[:, 0:4, 1:2], R2[:, 0:4, 1:2], R2[:, 4:8, 1:2], mx)
     for w in (2, 1):
-        tt(Z[:, 0, 0:w, 0:1], Z[:, 0, 0:w, 0:1], Z[:, 0, w:2 * w, 0:1], add)
-        tt(Z[:, 0, 0:w, 1:2], Z[:, 0, 0:w, 1:2], Z[:, 0, w:2 * w, 1:2], mx)
-    tt(T.SO[:], Z[:, 0, 0, :], T.SC[:], mul)
+        tt(FT[:, 0:w, 0:1], FT[:, 0:w, 0:1], FT[:, w:2 * w, 0:1], add)
+        tt(FT[:, 0:w, 1:2], FT[:, 0:w, 1:2], FT[:, w:2 * w, 1:2], mx)
+    tt(T.SO[:], FT[:, 0, 0:2], T.SC[:], mul)
     n_s = n[0]
 
-    g.sync.wait_ge(sem.v, n_y)
-    g.sync.dma_start(T.y[:, 2:2 + WI], T.Y[:]).then_inc(sem.st, 16)
-    g.scalar.wait_ge(sem.v, n_ye)
-    g.scalar.dma_start(T.y[:, W - 2:W], T.YE[:, 0:2]).then_inc(sem.st, 16)
-    g.scalar.dma_start(T.y[:, 0:2], T.YE[:, 2:4]).then_inc(sem.st, 16)
+    g.scalar.wait_ge(sem.v, n_d)
+    g.scalar.dma_start(T.RR[:, 0, :], D[:, W:W + 4]).then_inc(sem.l6, 16)
+    g.scalar.dma_start(T.LL[:, 5, :], D[:, 0:4]).then_inc(sem.l6, 16)
+    g.scalar.wait_ge(sem.v, n_y)
+    g.scalar.dma_start(T.y[:], T.Y[:]).then_inc(sem.st, 16)
     g.sync.wait_ge(sem.v, n_s)
     g.sync.dma_start(T.s[:], T.SO[:]).then_inc(sem.st, 16)
 
     left = 0
-    for ready, count, src, relay, hsem, slot, asem in (
-            (sem.le, 64, E[:, 0, :], T.RL1, sem.h1, _eslot, sem.a1),
-            (sem.v, n_msg2, Z[:, 6, 0, :], T.RL2, sem.h2, _zslot, sem.a2)):
-        g.wait_ge(ready, count)
-        if helpers:
-            left += _send(g, topo, core, src, helpers, [relay[:] for h in helpers], hsem, sem.ls)
-        if direct:
-            left += _send(g, topo, core, src, [cores[d] for d in direct],
-                          [slot(T, rank, d) for d in direct], asem, sem.ls)
+    dc = [cores[d] for d in direct]
+    g.wait_ge(sem.v, n_d)
+    if helpers:
+        left += _send(g, topo, core, [(D[:, W:W + 4], [T.RL1[:, 0, :] for h in helpers]),
+                                      (D[:, 0:4], [T.RL1[:, 1, :] for h in helpers])], helpers, sem.h1, sem.ls)
+    if direct:
+        left += _send(g, topo, core, _m1(T, D[:, W:W + 4], D[:, 0:4], rank, direct), dc, sem.a1, sem.ls)
+    g.wait_ge(sem.v, n_msg2)
+    if helpers:
+        left += _send(g, topo, core, [(R2[:, 0, :], [T.RL2[:] for h in helpers])], helpers, sem.h2, sem.ls)
+    if direct:
+        left += _send(g, topo, core, _m2(T, R2[:, 0, :], rank, direct), dc, sem.a2, sem.ls)
     g.wait_ge(sem.ls, left)
-    g.wait_ge(sem.st, 64)
+    g.wait_ge(sem.st, 32)

@@ -8,6 +8,7 @@ WD = W + 4
 WI = W - 4
 HW = WI // 2
 NSIM = 256
+K = 4
 
 F = "float32"
 SCRATCH = {
@@ -26,7 +27,7 @@ SCRATCH = {
     "SC": ("sbuf", [128, 2], F), "SO": ("sbuf", [128, 2], F),
     "RL1": ("sbuf", [128, 2, 4], F), "RL2": ("sbuf", [128, 4], F),
 }
-SEMAPHORES = ["lu", "lb", "l6", "i1", "i2", "pe", "v", "a1", "a2", "h1", "h2", "ls", "st"]
+SEMAPHORES = ["lu", "lb", "l6", "i1", "i2", "pe", "a1", "a2", "h1", "h2", "ls", "st"] + ["v%d" % i for i in range(K)]
 
 
 def _plan(T, topo):
@@ -107,23 +108,45 @@ def rank_program(g, core, T, topo):
     add, sub, mul, mx = AluOpType.add, AluOpType.subtract, AluOpType.mult, AluOpType.max
     vq = g.vector
     n = [0]
+    lastw, readers, waited = {}, {}, [0] * K
 
-    def chain():
-        if n[0]:
-            vq.wait_ge(sem.v, n[0])
+    def qwait(q, ids):
+        for i in ids:
+            q.wait_ge(sem["v%d" % (i % K)], i // K + 1)
+
+    def before(w, r):
+        i = n[0]
+        deps = set(readers.get(w, []))
+        for name in tuple(r) + (w,):
+            if name in lastw:
+                deps.add(lastw[name])
+        if i >= K:
+            deps.add(i - K)
+        for d in sorted(deps):
+            if d // K + 1 > waited[d % K]:
+                waited[d % K] = d // K + 1
+                qwait(vq, [d])
+        for name in r:
+            readers.setdefault(name, []).append(i)
+        lastw[w] = i
+        readers[w] = []
         n[0] += 1
+        return sem["v%d" % (i % K)]
 
-    def tt(out, a, b, op):
-        chain()
-        vq.tensor_tensor(out, a, b, op).then_inc(sem.v, 1)
+    def tt(w, r, out, a, b, op):
+        s = before(w, r)
+        vq.tensor_tensor(out, a, b, op).then_inc(s, 1)
+        return n[0] - 1
 
-    def fill(ap, c):
-        chain()
-        vq.memset(ap, c).then_inc(sem.v, 1)
+    def fill(w, ap, c):
+        s = before(w, ())
+        vq.memset(ap, c).then_inc(s, 1)
+        return n[0] - 1
 
-    def copy(out, in_):
-        chain()
-        vq.tensor_copy(out, in_).then_inc(sem.v, 1)
+    def copy(w, out, in_):
+        s = before(w, ())
+        vq.tensor_copy(out, in_).then_inc(s, 1)
+        return n[0] - 1
 
     arrive = 0
     for j in range(N):
@@ -138,117 +161,110 @@ def rank_program(g, core, T, topo):
                     arrive += _engines(topo, h, [cores[d] for d in s])
 
     UB, R2, A, ND, D, O, NO = T.UB, T.R2, T.A, T.ND, T.D, T.O, T.NO
-    U, B = UB[:, 0, :], UB[:, 1, :]
 
-    fill(T.Zi[:], 0.0)
-    fill(T.Zi[:, 0:1], 1.0)
-    n_zi = n[0]
-    fill(UB[:, :, 0:4], 0.0)
-    fill(UB[:, :, WP - 4:WP], 0.0)
-    fill(T.C8p[:, 0:WD], 8.0)
-    fill(T.C4p[:, 0:WD], 4.0)
-    fill(T.one[:], 1.0)
-    fill(R2[:, 0, 2:4], 0.0)
-    fill(O[:, 6:8, :], 0.0)
-    fill(T.NEG1[:], -1.0)
-    fill(T.c18[:], 0.125)
-    fill(T.SC[:, 0:1], -1.0 / (64.0 * N * W))
-    fill(T.SC[:, 1:2], 0.125)
+    fill("Zi", T.Zi[:], 0.0)
+    i_zi = fill("Zi", T.Zi[:, 0:1], 1.0)
+    fill("UB", UB[:, :, 0:4], 0.0)
+    fill("UB", UB[:, :, WP - 4:WP], 0.0)
+    fill("C8p", T.C8p[:, 0:WD], 8.0)
+    fill("C4p", T.C4p[:, 0:WD], 4.0)
+    i_one = fill("one", T.one[:], 1.0)
+    i_pad = fill("R2p", R2[:, 0, 2:4], 0.0)
+    fill("O", O[:, 6:8, :], 0.0)
+    fill("NEG1", T.NEG1[:], -1.0)
+    fill("c18", T.c18[:], 0.125)
+    fill("SC", T.SC[:, 0:1], -1.0 / (64.0 * N * W))
+    fill("SC", T.SC[:, 1:2], 0.125)
 
     g.sync.dma_start(UB[0:64, 0, 4:4 + W], T.u[0:64, :]).then_inc(sem.lu, 16)
     g.scalar.dma_start(UB[64:128, 0, 4:4 + W], T.u[64:128, :]).then_inc(sem.lu, 16)
     g.sync.dma_start(UB[0:64, 1, 4:4 + W], T.b[0:64, :]).then_inc(sem.lb, 16)
     g.scalar.dma_start(UB[64:128, 1, 4:4 + W], T.b[64:128, :]).then_inc(sem.lb, 16)
-    g.sync.wait_ge(sem.v, n_zi)
+    qwait(g.sync, [i_zi])
     g.sync.dma_start(T.IDd[:], T.Zi[:]).then_inc(sem.i1, 16)
     g.sync.wait_ge(sem.i1, 16)
     g.sync.dma_start(T.I[:], T.IDd[0:128 * 128]).then_inc(sem.i2, 16)
 
     a = A[:, 0:WD]
     vq.wait_ge(sem.lu, 32)
-    tt(T.Pm[:, 0:WP - 1], UB[:, 0, 0:WP - 1], UB[:, 0, 1:WP], add)
-    tt(a, T.Pm[:, 0:WD], T.Pm[:, 3:3 + WD], add)
-    tt(T.u8[:], UB[:, 0, 2:2 + WD], T.C8p[:, 0:WD], mul)
+    tt("Pm", ("UB",), T.Pm[:, 0:WP - 1], UB[:, 0, 0:WP - 1], UB[:, 0, 1:WP], add)
+    tt("u8", ("UB", "C8p"), T.u8[:], UB[:, 0, 2:2 + WD], T.C8p[:, 0:WD], mul)
     vq.wait_ge(sem.lb, 32)
-    tt(T.b4[:], UB[:, 1, 2:2 + WD], T.C4p[:, 0:WD], mul)
-    tt(a, a, T.b4[:], add)
-    tt(D[:], a, T.u8[:], sub)
-    n_d = n[0]
-    tt(ND[:, 0:WI], T.u8[:, 4:4 + WI], A[:, 4:4 + WI], sub)
-    tt(T.SQ[:], D[:, 4:4 + WI], ND[:, 0:WI], mul)
-    n_sq = n[0]
+    tt("b4", ("UB", "C4p"), T.b4[:], UB[:, 1, 2:2 + WD], T.C4p[:, 0:WD], mul)
+    tt("A", ("Pm",), a, T.Pm[:, 0:WD], T.Pm[:, 3:3 + WD], add)
+    tt("A", ("A", "b4"), a, a, T.b4[:], add)
+    i_d = tt("D", ("A", "u8"), D[:], a, T.u8[:], sub)
+    tt("ND", ("A", "u8"), ND[:, 0:WI], T.u8[:, 4:4 + WI], A[:, 4:4 + WI], sub)
+    i_sq = tt("SQ", ("D", "ND"), T.SQ[:], D[:, 4:4 + WI], ND[:, 0:WI], mul)
     ABl, ABh = T.ABl, T.ABh[:, 0:HW]
-    tt(ABl[:], D[:, 4:4 + HW], ND[:, 0:HW], mx)
-    tt(ABh, D[:, 4 + HW:4 + WI], ND[:, HW:WI], mx)
-    tt(ABl[:], ABl[:], ABh, mx)
-    tt(ABl[:, 0:63], ABl[:, 0:63], ABl[:, 63:126], mx)
-    tt(ABl[:, 0:31], ABl[:, 0:31], ABl[:, 32:63], mx)
-    tt(ABl[:, 0:16], ABl[:, 0:16], ABl[:, 16:32], mx)
+    tt("ABl", ("D", "ND"), ABl[:], D[:, 4:4 + HW], ND[:, 0:HW], mx)
+    tt("ABh", ("D", "ND"), ABh, D[:, 4 + HW:4 + WI], ND[:, HW:WI], mx)
+    tt("ABl", ("ABl", "ABh"), ABl[:], ABl[:], ABh, mx)
+    tt("ABl", ("ABl",), ABl[:, 0:63], ABl[:, 0:63], ABl[:, 63:126], mx)
+    tt("ABl", ("ABl",), ABl[:, 0:31], ABl[:, 0:31], ABl[:, 32:63], mx)
+    tt("ABl", ("ABl",), ABl[:, 0:16], ABl[:, 0:16], ABl[:, 16:32], mx)
     vq.wait_ge(sem.pe, 1)
-    copy(T.Ts[0:HW, :], T.TP[0:HW, 0:128])
-    n_ts = n[0]
+    i_ts = copy("Ts", T.Ts[0:HW, :], T.TP[0:HW, 0:128])
     for w in (8, 4, 2):
-        tt(ABl[:, 0:w], ABl[:, 0:w], ABl[:, w:2 * w], mx)
-    tt(R2[:, 0, 1:2], ABl[:, 0:1], ABl[:, 1:2], mx)
+        tt("ABl", ("ABl",), ABl[:, 0:w], ABl[:, 0:w], ABl[:, w:2 * w], mx)
+    i_m = tt("R2m", ("ABl",), R2[:, 0, 1:2], ABl[:, 0:1], ABl[:, 1:2], mx)
     vq.wait_ge(sem.pe, 2)
-    copy(R2[:, 0, 0:1], T.SP[:, 0:1])
-    n_msg2 = n[0]
+    i_s = copy("R2s", R2[:, 0, 0:1], T.SP[:, 0:1])
 
     tq = g.tensor
     tq.wait_ge(sem.i2, 16)
-    tq.wait_ge(sem.v, n_sq)
+    qwait(tq, [i_sq])
     tq.matmul(T.TP[0:HW, 0:128], T.SQ[:, 0:HW], T.I[:], True, False)
     tq.matmul(T.TP[0:HW, 0:128], T.SQ[:, HW:WI], T.I[:], False, True).then_inc(sem.pe, 1)
-    tq.wait_ge(sem.v, n_ts)
+    qwait(tq, [i_one, i_ts])
     tq.matmul(T.SP[:, 0:1], T.Ts[0:HW, :], T.one[0:HW, :], True, True).then_inc(sem.pe, 1)
 
+    ABe, SQe = T.ABe, T.SQe
     vq.wait_ge(sem.l6, 32)
     vq.wait_ge(sem.a1, arrive)
-    tt(O[:, 0:6, :], T.RR[:], T.LL[:], add)
-    tt(A[:, 2:4], O[:, 5, 2:4], T.u8[:, 2:4], add)
-    tt(A[:, W:W + 2], O[:, 0, 0:2], T.u8[:, W:W + 2], add)
-    tt(T.Y[:], A[:, 2:2 + W], T.c18[:], mul)
-    n_y = n[0]
-    ABe, SQe = T.ABe, T.SQe
-    tt(NO[:], O[:], T.NEG1[:], mul)
-    tt(ABe[:], O[:], NO[:], mx)
-    tt(SQe[:], O[:], NO[:], mul)
+    tt("O", (), O[:, 0:6, :], T.RR[:], T.LL[:], add)
+    tt("NO", ("O", "NEG1"), NO[:], O[:], T.NEG1[:], mul)
+    tt("A", ("O", "u8"), A[:, 2:4], O[:, 5, 2:4], T.u8[:, 2:4], add)
+    tt("A", ("O", "u8"), A[:, W:W + 2], O[:, 0, 0:2], T.u8[:, W:W + 2], add)
+    tt("ABe", ("O", "NO"), ABe[:], O[:], NO[:], mx)
+    tt("SQe", ("O", "NO"), SQe[:], O[:], NO[:], mul)
+    i_y = tt("Y", ("A", "c18"), T.Y[:], A[:, 2:2 + W], T.c18[:], mul)
     for w in (4, 2, 1):
-        tt(ABe[:, 0:w, :], ABe[:, 0:w, :], ABe[:, w:2 * w, :], mx)
-        tt(SQe[:, 0:w, :], SQe[:, 0:w, :], SQe[:, w:2 * w, :], add)
-    tt(R2[:, 6:8, 1], ABe[:, 0, 0:2], ABe[:, 0, 2:4], mx)
-    tt(R2[:, 6:8, 0], SQe[:, 0, 0:2], SQe[:, 0, 2:4], add)
+        tt("ABe", ("ABe",), ABe[:, 0:w, :], ABe[:, 0:w, :], ABe[:, w:2 * w, :], mx)
+        tt("SQe", ("SQe",), SQe[:, 0:w, :], SQe[:, 0:w, :], SQe[:, w:2 * w, :], add)
+    tt("R2m", ("ABe",), R2[:, 6:8, 1], ABe[:, 0, 0:2], ABe[:, 0, 2:4], mx)
+    tt("R2s", ("SQe",), R2[:, 6:8, 0], SQe[:, 0, 0:2], SQe[:, 0, 2:4], add)
 
     FT = T.FT
     vq.wait_ge(sem.a2, arrive)
-    tt(FT[:, 0:4, 0:1], R2[:, 0:4, 0:1], R2[:, 4:8, 0:1], add)
-    tt(FT[:, 0:4, 1:2], R2[:, 0:4, 1:2], R2[:, 4:8, 1:2], mx)
+    tt("FTs", ("R2s",), FT[:, 0:4, 0:1], R2[:, 0:4, 0:1], R2[:, 4:8, 0:1], add)
+    tt("FTm", ("R2m",), FT[:, 0:4, 1:2], R2[:, 0:4, 1:2], R2[:, 4:8, 1:2], mx)
     for w in (2, 1):
-        tt(FT[:, 0:w, 0:1], FT[:, 0:w, 0:1], FT[:, w:2 * w, 0:1], add)
-        tt(FT[:, 0:w, 1:2], FT[:, 0:w, 1:2], FT[:, w:2 * w, 1:2], mx)
-    tt(T.SO[:], FT[:, 0, 0:2], T.SC[:], mul)
-    n_s = n[0]
+        tt("FTs", ("FTs",), FT[:, 0:w, 0:1], FT[:, 0:w, 0:1], FT[:, w:2 * w, 0:1], add)
+        tt("FTm", ("FTm",), FT[:, 0:w, 1:2], FT[:, 0:w, 1:2], FT[:, w:2 * w, 1:2], mx)
+    i_so = tt("SO", ("FTs", "FTm", "SC"), T.SO[:], FT[:, 0, 0:2], T.SC[:], mul)
 
-    g.scalar.wait_ge(sem.v, n_d)
+    qwait(g.scalar, [i_d])
     g.scalar.dma_start(T.RR[:, 0, :], D[:, W:W + 4]).then_inc(sem.l6, 16)
     g.scalar.dma_start(T.LL[:, 5, :], D[:, 0:4]).then_inc(sem.l6, 16)
-    g.scalar.wait_ge(sem.v, n_y)
+    qwait(g.scalar, [i_y])
     g.scalar.dma_start(T.y[:], T.Y[:]).then_inc(sem.st, 16)
-    g.sync.wait_ge(sem.v, n_s)
+    qwait(g.sync, [i_so])
     g.sync.dma_start(T.s[:], T.SO[:]).then_inc(sem.st, 16)
 
     left = 0
     dc = [cores[d] for d in direct]
-    g.wait_ge(sem.v, n_d)
+    qwait(g, [i_d])
     if helpers:
         left += _send(g, topo, core, [(D[:, W:W + 4], [T.RL1[:, 0, :] for h in helpers]),
                                       (D[:, 0:4], [T.RL1[:, 1, :] for h in helpers])], helpers, sem.h1, sem.ls)
     if direct:
         left += _send(g, topo, core, _m1(T, D[:, W:W + 4], D[:, 0:4], rank, direct), dc, sem.a1, sem.ls)
-    g.wait_ge(sem.v, n_msg2)
+    qwait(g, [i_pad, i_m, i_s])
     if helpers:
         left += _send(g, topo, core, [(R2[:, 0, :], [T.RL2[:] for h in helpers])], helpers, sem.h2, sem.ls)
     if direct:
         left += _send(g, topo, core, _m2(T, R2[:, 0, :], rank, direct), dc, sem.a2, sem.ls)
     g.wait_ge(sem.ls, left)
     g.wait_ge(sem.st, 32)
+    qwait(g, range(n[0] - K, n[0]))

@@ -1,33 +1,32 @@
+import math
 from concourse.bass import DstId, RemoteDMATransfer
-from concourse.mybir import AluOpType
+from concourse.mybir import AluOpType, AxisListType, ActivationFunctionType
 
 N = 6
 W = 256
-WP = W + 8
-WD = W + 4
 WI = W - 4
-HW = WI // 2
 NSIM = 256
-K = 4
+NC = 44
+M1 = 8
+M2 = 2
+R2O = 8
 
 F = "float32"
 SCRATCH = {
-    "UB": ("sbuf", [128, 2, WP], F), "Pm": ("sbuf", [128, WP], F),
-    "b4": ("sbuf", [128, WD], F), "u8": ("sbuf", [128, WD], F), "D": ("sbuf", [128, WD], F),
-    "ABl": ("sbuf", [128, HW], F), "SQ": ("sbuf", [128, WI], F),
-    "Y": ("sbuf", [128, W], F), "c18": ("sbuf", [128, W], F),
-    "C4p": ("psum", [128, 512], F), "C8p": ("psum", [128, 512], F), "A": ("psum", [128, 512], F),
-    "ND": ("psum", [128, 512], F), "ABh": ("psum", [128, 512], F), "TP": ("psum", [128, 512], F), "SP": ("psum", [128, 512], F),
-    "Zi": ("sbuf", [128, 129], F), "IDd": ("dram", [128 * 129], F), "I": ("sbuf", [128, 128], F),
-    "Ts": ("sbuf", [128, 128], F), "one": ("sbuf", [128, 1], F),
-    "RR": ("sbuf", [128, 6, 4], F), "LL": ("sbuf", [128, 6, 4], F),
-    "O": ("sbuf", [128, 8, 4], F), "NO": ("sbuf", [128, 8, 4], F), "NEG1": ("sbuf", [128, 8, 4], F),
-    "ABe": ("sbuf", [128, 8, 4], F), "SQe": ("sbuf", [128, 8, 4], F),
-    "R2": ("sbuf", [128, 8, 4], F), "FT": ("sbuf", [128, 4, 4], F),
-    "SC": ("sbuf", [128, 2], F), "SO": ("sbuf", [128, 2], F),
-    "RL1": ("sbuf", [128, 2, 4], F), "RL2": ("sbuf", [128, 4], F),
+    "E": ("sbuf", [128, 2, 12], F),
+    "Q": ("sbuf", [128, 12], F), "HB": ("sbuf", [128, 8], F), "PE": ("sbuf", [128, 11], F),
+    "TE": ("sbuf", [128, 8], F), "AE": ("sbuf", [128, 8], F), "YE": ("sbuf", [128, 8], F),
+    "UB": ("sbuf", [128, W], F), "BB": ("sbuf", [128, W], F),
+    "P": ("sbuf", [128, W], F), "A": ("sbuf", [128, WI], F), "Y8": ("sbuf", [128, WI], F), "D": ("sbuf", [128, WI], F),
+    "SQ": ("sbuf", [128, WI], F), "Y": ("sbuf", [128, WI], F),
+    "U8": ("psum", [128, 512], F), "B4": ("psum", [128, 512], F),
+    "R1": ("sbuf", [128, 7 * M1], F),
+    "R2": ("sbuf", [128, 20], F),
+    "O": ("sbuf", [128, 24], F), "SO2": ("sbuf", [128, 24], F), "MO": ("sbuf", [128, 1], F), "MX": ("sbuf", [128, 1], F),
+    "YR": ("sbuf", [128, 2], F), "YL": ("sbuf", [128, 2], F), "SO": ("sbuf", [128, 2], F),
+    "RL1": ("sbuf", [128, M1], F), "RL2": ("sbuf", [128, M2], F),
 }
-SEMAPHORES = ["lu", "lb", "l6", "i1", "i2", "pe", "a1", "a2", "h1", "h2", "ls", "st"] + ["v%d" % i for i in range(K)]
+SEMAPHORES = ["leu", "leb", "lu", "lb", "a1", "a2", "h1", "h2", "ls", "st"] + ["c%d" % i for i in range(NC)]
 
 
 def _plan(T, topo):
@@ -53,43 +52,47 @@ def _mask(topo, src, dsts):
     return m
 
 
-def _engines(topo, src, dsts):
-    return bin(_mask(topo, src, dsts)).count("1")
+def _count(m):
+    return bin(m).count("1")
 
 
-def _send(g, topo, src, parts, dsts, remote_sem, local_sem):
-    ids = []
+def _ids(topo, src, dsts):
+    out = []
     for d in dsts:
         rid, pid = topo.addr(d, src)
-        ids.append(DstId(rid=rid, pnc=pid))
-    m = _mask(topo, src, dsts)
-    bits = [1 << i for i in range(m.bit_length()) if (m >> i) & 1]
-    k = len(bits) // len(parts)
-    trs = []
-    for i, (s_ap, d_aps) in enumerate(parts):
-        trs.append(RemoteDMATransfer(dst_ids=ids, dma_engine_mask=sum(bits[i * k:(i + 1) * k]), remote_sem=remote_sem,
-                                     srcs=[s_ap], dsts=list(d_aps), alu_op=0))
-    g.remote_dma_fused(trs, local_sem=local_sem)
-    return k * len(parts)
+        out.append(DstId(rid=rid, pnc=pid))
+    return out
 
 
-def _m1(T, right, left, j, ds):
-    return [(right, [T.RR[:, (j - d) % N, :] for d in ds]), (left, [T.LL[:, (j - d) % N - 1, :] for d in ds])]
+def _rank_masks(topo, cores, plan, j):
+    direct, helpers, share = plan[j]
+    off = _mask(topo, cores[j], [cores[d] for d in direct]) if direct else 0
+    on = _mask(topo, cores[j], helpers) if helpers else 0
+    return on & ~off, off
 
 
-def _m2(T, src, j, ds):
-    return [(src, [T.R2[:, (j - d) % N, :] for d in ds])]
+def _slot1(T, j, d):
+    k = (j - d) % N
+    return T.R1[:, M1 * k:M1 * k + M1]
+
+
+def _slot2(T, j, d):
+    k = (j - d) % N
+    return T.R2[:, R2O + M2 * (k - 1):R2O + M2 * k]
 
 
 def _carrier(g, core, T, topo, j, share, n_in):
     cores = list(T.cores)
     dsts = [cores[d] for d in share]
-    left = 0
+    m = _mask(topo, core, dsts)
+    ids = _ids(topo, core, dsts)
     g.wait_ge(T.sem.h1, n_in)
-    left += _send(g, topo, core, _m1(T, T.RL1[:, 0, :], T.RL1[:, 1, :], j, share), dsts, T.sem.a1, T.sem.ls)
+    g.remote_dma_fused([RemoteDMATransfer(dst_ids=ids, dma_engine_mask=m, remote_sem=T.sem.a1, srcs=[T.RL1[:]],
+                                          dsts=[_slot1(T, j, d) for d in share], alu_op=0)], local_sem=T.sem.ls)
     g.wait_ge(T.sem.h2, n_in)
-    left += _send(g, topo, core, _m2(T, T.RL2[:], j, share), dsts, T.sem.a2, T.sem.ls)
-    g.wait_ge(T.sem.ls, left)
+    g.remote_dma_fused([RemoteDMATransfer(dst_ids=ids, dma_engine_mask=m, remote_sem=T.sem.a2, srcs=[T.RL2[:]],
+                                          dsts=[_slot2(T, j, d) for d in share], alu_op=0)], local_sem=T.sem.ls)
+    g.wait_ge(T.sem.ls, 2 * _count(m))
 
 
 def rank_program(g, core, T, topo):
@@ -100,53 +103,38 @@ def rank_program(g, core, T, topo):
         for j in range(N):
             direct, helpers, share = plan[j]
             if core in helpers:
-                _carrier(g, core, T, topo, j, share[helpers.index(core)], _engines(topo, cores[j], helpers))
+                _carrier(g, core, T, topo, j, share[helpers.index(core)], _count(_rank_masks(topo, cores, plan, j)[0]))
         return
 
     direct, helpers, share = plan[rank]
     sem = T.sem
     add, sub, mul, mx = AluOpType.add, AluOpType.subtract, AluOpType.mult, AluOpType.max
-    vq = g.vector
-    n = [0]
-    lastw, readers, waited = {}, {}, [0] * K
+    X = AxisListType.X
+    Copy, Square = ActivationFunctionType.Copy, ActivationFunctionType.Square
+    vq, sq, yq = g.vector, g.scalar, g.sync
+    nid = [0]
+    waited = {}
+    consumed = set()
 
-    def qwait(q, ids):
+    def need(q, name, ids):
+        seen = waited.setdefault(name, set())
         for i in ids:
-            q.wait_ge(sem["v%d" % (i % K)], i // K + 1)
+            if i not in seen:
+                q.wait_ge(sem["c%d" % i], 1)
+                seen.add(i)
+                consumed.add(i)
 
-    def before(w, r):
-        i = n[0]
-        deps = set(readers.get(w, []))
-        for name in tuple(r) + (w,):
-            if name in lastw:
-                deps.add(lastw[name])
-        if i >= K:
-            deps.add(i - K)
-        for d in sorted(deps):
-            if d // K + 1 > waited[d % K]:
-                waited[d % K] = d // K + 1
-                qwait(vq, [d])
-        for name in r:
-            readers.setdefault(name, []).append(i)
-        lastw[w] = i
-        readers[w] = []
-        n[0] += 1
-        return sem["v%d" % (i % K)]
+    def done(instr):
+        i = nid[0]
+        instr.then_inc(sem["c%d" % i], 1)
+        nid[0] += 1
+        return i
 
-    def tt(w, r, out, a, b, op):
-        s = before(w, r)
-        vq.tensor_tensor(out, a, b, op).then_inc(s, 1)
-        return n[0] - 1
+    def V(ids):
+        need(vq, "v", ids)
 
-    def fill(w, ap, c):
-        s = before(w, ())
-        vq.memset(ap, c).then_inc(s, 1)
-        return n[0] - 1
-
-    def copy(w, out, in_):
-        s = before(w, ())
-        vq.tensor_copy(out, in_).then_inc(s, 1)
-        return n[0] - 1
+    def S(ids):
+        need(sq, "s", ids)
 
     arrive = 0
     for j in range(N):
@@ -154,117 +142,114 @@ def rank_program(g, core, T, topo):
             continue
         dj, hj, sj = plan[j]
         if rank in dj:
-            arrive += _engines(topo, cores[j], [cores[d] for d in dj])
+            arrive += _count(_rank_masks(topo, cores, plan, j)[1])
         else:
             for h, s in zip(hj, sj):
                 if rank in s:
-                    arrive += _engines(topo, h, [cores[d] for d in s])
+                    arrive += _count(_mask(topo, h, [cores[d] for d in s]))
 
-    UB, R2, A, ND, D, O, NO = T.UB, T.R2, T.A, T.ND, T.D, T.O, T.NO
+    E, R1, R2, O = T.E, T.R1, T.R2, T.O
+    c1 = 1.0 / math.sqrt(float(N * W))
 
-    fill("Zi", T.Zi[:], 0.0)
-    i_zi = fill("Zi", T.Zi[:, 0:1], 1.0)
-    fill("UB", UB[:, :, 0:4], 0.0)
-    fill("UB", UB[:, :, WP - 4:WP], 0.0)
-    fill("C8p", T.C8p[:, 0:WD], 8.0)
-    fill("C4p", T.C4p[:, 0:WD], 4.0)
-    i_one = fill("one", T.one[:], 1.0)
-    i_pad = fill("R2p", R2[:, 0, 2:4], 0.0)
-    fill("O", O[:, 6:8, :], 0.0)
-    fill("NEG1", T.NEG1[:], -1.0)
-    fill("c18", T.c18[:], 0.125)
-    fill("SC", T.SC[:, 0:1], -1.0 / (64.0 * N * W))
-    fill("SC", T.SC[:, 1:2], 0.125)
+    yq.dma_start(E[:, 0, 0:4], T.u[:, W - 4:W]).then_inc(sem.leu, 16)
+    sq.dma_start(E[:, 0, 8:12], T.u[:, 0:4]).then_inc(sem.leu, 16)
+    yq.dma_start(E[:, 1, 0:4], T.b[:, W - 4:W]).then_inc(sem.leb, 16)
+    sq.dma_start(E[:, 1, 8:12], T.b[:, 0:4]).then_inc(sem.leb, 16)
+    yq.dma_start(T.UB[0:64, :], T.u[0:64, :]).then_inc(sem.lu, 16)
+    sq.dma_start(T.UB[64:128, :], T.u[64:128, :]).then_inc(sem.lu, 16)
+    yq.dma_start(T.BB[0:64, :], T.b[0:64, :]).then_inc(sem.lb, 16)
+    sq.dma_start(T.BB[64:128, :], T.b[64:128, :]).then_inc(sem.lb, 16)
 
-    g.sync.dma_start(UB[0:64, 0, 4:4 + W], T.u[0:64, :]).then_inc(sem.lu, 16)
-    g.scalar.dma_start(UB[64:128, 0, 4:4 + W], T.u[64:128, :]).then_inc(sem.lu, 16)
-    g.sync.dma_start(UB[0:64, 1, 4:4 + W], T.b[0:64, :]).then_inc(sem.lb, 16)
-    g.scalar.dma_start(UB[64:128, 1, 4:4 + W], T.b[64:128, :]).then_inc(sem.lb, 16)
-    qwait(g.sync, [i_zi])
-    g.sync.dma_start(T.IDd[:], T.Zi[:]).then_inc(sem.i1, 16)
-    g.sync.wait_ge(sem.i1, 16)
-    g.sync.dma_start(T.I[:], T.IDd[0:128 * 128]).then_inc(sem.i2, 16)
+    f_e = done(vq.memset(E[:, :, 4:8], 0.0))
+    f_a = done(vq.memset(R2[:, 2:4], 0.0))
+    f_b = done(vq.memset(R2[:, 5:8], 0.0))
 
-    a = A[:, 0:WD]
+    S([f_e])
+    sq.wait_ge(sem.leu, 32)
+    i_q = done(sq.activation(T.Q[:], E[:, 0, :], Copy, scale=0.125))
+    V([f_e])
+    vq.wait_ge(sem.leb, 32)
+    i_hb = done(vq.tensor_scalar(T.HB[:], E[:, 1, 2:10], 0.5, None, mul))
+    V([i_q])
+    i_pe = done(vq.tensor_tensor(T.PE[:], T.Q[:, 0:11], T.Q[:, 1:12], add))
+    V([i_hb])
+    vq.wait_ge(sem.leu, 32)
+    i_te = done(vq.tensor_tensor(T.TE[:], T.HB[:], E[:, 0, 2:10], sub))
+    V([i_pe])
+    i_ae = done(vq.tensor_tensor(T.AE[:], T.PE[:, 0:8], T.PE[:, 3:11], add))
+    V([i_ae, i_te])
+    i_de = done(vq.tensor_tensor(R1[:, 0:M1], T.AE[:], T.TE[:], add))
+
+    sq.wait_ge(sem.lu, 32)
+    i_u8 = done(sq.activation(T.U8[:, 0:WI], T.UB[:, 2:2 + WI], Copy, scale=8.0))
+    sq.wait_ge(sem.lb, 32)
+    i_b4 = done(sq.activation(T.B4[:, 0:WI], T.BB[:, 2:2 + WI], Copy, scale=4.0))
     vq.wait_ge(sem.lu, 32)
-    tt("Pm", ("UB",), T.Pm[:, 0:WP - 1], UB[:, 0, 0:WP - 1], UB[:, 0, 1:WP], add)
-    tt("u8", ("UB", "C8p"), T.u8[:], UB[:, 0, 2:2 + WD], T.C8p[:, 0:WD], mul)
-    vq.wait_ge(sem.lb, 32)
-    tt("b4", ("UB", "C4p"), T.b4[:], UB[:, 1, 2:2 + WD], T.C4p[:, 0:WD], mul)
-    tt("A", ("Pm",), a, T.Pm[:, 0:WD], T.Pm[:, 3:3 + WD], add)
-    tt("A", ("A", "b4"), a, a, T.b4[:], add)
-    i_d = tt("D", ("A", "u8"), D[:], a, T.u8[:], sub)
-    tt("ND", ("A", "u8"), ND[:, 0:WI], T.u8[:, 4:4 + WI], A[:, 4:4 + WI], sub)
-    i_sq = tt("SQ", ("D", "ND"), T.SQ[:], D[:, 4:4 + WI], ND[:, 0:WI], mul)
-    ABl, ABh = T.ABl, T.ABh[:, 0:HW]
-    tt("ABl", ("D", "ND"), ABl[:], D[:, 4:4 + HW], ND[:, 0:HW], mx)
-    tt("ABh", ("D", "ND"), ABh, D[:, 4 + HW:4 + WI], ND[:, HW:WI], mx)
-    tt("ABl", ("ABl", "ABh"), ABl[:], ABl[:], ABh, mx)
-    tt("ABl", ("ABl",), ABl[:, 0:63], ABl[:, 0:63], ABl[:, 63:126], mx)
-    tt("ABl", ("ABl",), ABl[:, 0:31], ABl[:, 0:31], ABl[:, 32:63], mx)
-    tt("ABl", ("ABl",), ABl[:, 0:16], ABl[:, 0:16], ABl[:, 16:32], mx)
-    vq.wait_ge(sem.pe, 1)
-    i_ts = copy("Ts", T.Ts[0:HW, :], T.TP[0:HW, 0:128])
-    for w in (8, 4, 2):
-        tt("ABl", ("ABl",), ABl[:, 0:w], ABl[:, 0:w], ABl[:, w:2 * w], mx)
-    i_m = tt("R2m", ("ABl",), R2[:, 0, 1:2], ABl[:, 0:1], ABl[:, 1:2], mx)
-    vq.wait_ge(sem.pe, 2)
-    i_s = copy("R2s", R2[:, 0, 0:1], T.SP[:, 0:1])
+    i_p = done(vq.tensor_tensor(T.P[:, 0:W - 1], T.UB[:, 0:W - 1], T.UB[:, 1:W], add))
+    V([i_p])
+    i_a = done(vq.tensor_tensor(T.A[:], T.P[:, 0:WI], T.P[:, 3:3 + WI], add))
+    V([i_a, i_b4])
+    i_y8 = done(vq.tensor_tensor(T.Y8[:], T.A[:], T.B4[:, 0:WI], add))
+    V([i_y8, i_u8])
+    i_d = done(vq.tensor_tensor(T.D[:], T.Y8[:], T.U8[:, 0:WI], sub))
+    V([i_d])
+    i_m = done(vq.tensor_reduce(R2[:, 1:2], T.D[:], X, mx, apply_absolute_value=True))
+    S([i_d])
+    i_s = done(sq.activation(T.SQ[:], T.D[:], Square, scale=c1 / 8.0, accum_out=R2[:, 0:1]))
+    S([i_y8])
+    i_y = done(sq.activation(T.Y[:], T.Y8[:], Copy, scale=0.125))
 
-    tq = g.tensor
-    tq.wait_ge(sem.i2, 16)
-    qwait(tq, [i_sq])
-    tq.matmul(T.TP[0:HW, 0:128], T.SQ[:, 0:HW], T.I[:], True, False)
-    tq.matmul(T.TP[0:HW, 0:128], T.SQ[:, HW:WI], T.I[:], False, True).then_inc(sem.pe, 1)
-    qwait(tq, [i_one, i_ts])
-    tq.matmul(T.SP[:, 0:1], T.Ts[0:HW, :], T.one[0:HW, :], True, True).then_inc(sem.pe, 1)
+    i_d6 = done(vq.tensor_tensor(R1[:, 6 * M1:7 * M1], T.AE[:], T.TE[:], add))
+    i_ye = done(vq.tensor_tensor(T.YE[:], T.AE[:], T.HB[:], add))
 
-    ABe, SQe = T.ABe, T.SQe
-    vq.wait_ge(sem.l6, 32)
     vq.wait_ge(sem.a1, arrive)
-    tt("O", (), O[:, 0:6, :], T.RR[:], T.LL[:], add)
-    tt("NO", ("O", "NEG1"), NO[:], O[:], T.NEG1[:], mul)
-    tt("A", ("O", "u8"), A[:, 2:4], O[:, 5, 2:4], T.u8[:, 2:4], add)
-    tt("A", ("O", "u8"), A[:, W:W + 2], O[:, 0, 0:2], T.u8[:, W:W + 2], add)
-    tt("ABe", ("O", "NO"), ABe[:], O[:], NO[:], mx)
-    tt("SQe", ("O", "NO"), SQe[:], O[:], NO[:], mul)
-    i_y = tt("Y", ("A", "c18"), T.Y[:], A[:, 2:2 + W], T.c18[:], mul)
-    for w in (4, 2, 1):
-        tt("ABe", ("ABe",), ABe[:, 0:w, :], ABe[:, 0:w, :], ABe[:, w:2 * w, :], mx)
-        tt("SQe", ("SQe",), SQe[:, 0:w, :], SQe[:, 0:w, :], SQe[:, w:2 * w, :], add)
-    tt("R2m", ("ABe",), R2[:, 6:8, 1], ABe[:, 0, 0:2], ABe[:, 0, 2:4], mx)
-    tt("R2s", ("SQe",), R2[:, 6:8, 0], SQe[:, 0, 0:2], SQe[:, 0, 2:4], add)
+    V([i_de, i_d6])
+    i_o = [done(vq.tensor_tensor(O[:, 6 * j:6 * j + 6], R1[:, j:6 * M1:M1], R1[:, M1 + 4 + j:7 * M1:M1], add))
+           for j in range(4)]
+    V([i_ye])
+    i_yr = done(vq.tensor_tensor(T.YR[:], T.YE[:, 0:2], R1[:, M1 + 4:M1 + 6], add))
+    i_yl = done(vq.tensor_tensor(T.YL[:], T.YE[:, 6:8], R1[:, 5 * M1 + 2:5 * M1 + 4], add))
+    V(i_o)
+    i_mo = done(vq.tensor_reduce(T.MO[:], O[:], X, mx, apply_absolute_value=True))
+    S(i_o + [f_b])
+    i_so = done(sq.activation(T.SO2[:], O[:], Square, scale=c1, accum_out=R2[:, 4:5]))
 
-    FT = T.FT
     vq.wait_ge(sem.a2, arrive)
-    tt("FTs", ("R2s",), FT[:, 0:4, 0:1], R2[:, 0:4, 0:1], R2[:, 4:8, 0:1], add)
-    tt("FTm", ("R2m",), FT[:, 0:4, 1:2], R2[:, 0:4, 1:2], R2[:, 4:8, 1:2], mx)
-    for w in (2, 1):
-        tt("FTs", ("FTs",), FT[:, 0:w, 0:1], FT[:, 0:w, 0:1], FT[:, w:2 * w, 0:1], add)
-        tt("FTm", ("FTm",), FT[:, 0:w, 1:2], FT[:, 0:w, 1:2], FT[:, w:2 * w, 1:2], mx)
-    i_so = tt("SO", ("FTs", "FTm", "SC"), T.SO[:], FT[:, 0, 0:2], T.SC[:], mul)
+    V([i_m, f_a, f_b])
+    i_f1 = done(vq.tensor_reduce(T.MX[:], R2[:, 1:R2O + 5 * M2:2], X, mx))
+    V([i_s, i_so])
+    i_f2 = done(vq.tensor_reduce(T.SO[:, 0:1], R2[:, 0:R2O + 5 * M2:2], X, add))
+    V([i_f1, i_mo])
+    i_f3 = done(vq.tensor_scalar(T.SO[:, 1:2], T.MX[:], 0.125, T.MO[:], mul, mx))
 
-    qwait(g.scalar, [i_d])
-    g.scalar.dma_start(T.RR[:, 0, :], D[:, W:W + 4]).then_inc(sem.l6, 16)
-    g.scalar.dma_start(T.LL[:, 5, :], D[:, 0:4]).then_inc(sem.l6, 16)
-    qwait(g.scalar, [i_y])
-    g.scalar.dma_start(T.y[:], T.Y[:]).then_inc(sem.st, 16)
-    qwait(g.sync, [i_so])
-    g.sync.dma_start(T.s[:], T.SO[:]).then_inc(sem.st, 16)
+    need(yq, "y", [i_y])
+    yq.dma_start(T.y[:, 2:2 + WI], T.Y[:]).then_inc(sem.st, 16)
+    need(yq, "y", [i_yr])
+    yq.dma_start(T.y[:, W - 2:W], T.YR[:]).then_inc(sem.st, 16)
+    S([i_yl])
+    sq.dma_start(T.y[:, 0:2], T.YL[:]).then_inc(sem.st, 16)
+    need(yq, "y", [i_f2, i_f3])
+    yq.dma_start(T.s[:], T.SO[:]).then_inc(sem.st, 16)
+
+    cm, om = _rank_masks(topo, cores, plan, rank)
+    dc = [cores[d] for d in direct]
+
+    def send(src, hbuf, hsem, slot, asem):
+        trs = []
+        if helpers:
+            trs.append(RemoteDMATransfer(dst_ids=_ids(topo, core, helpers), dma_engine_mask=cm, remote_sem=hsem,
+                                         srcs=[src], dsts=[hbuf[:] for h in helpers], alu_op=0))
+        if direct:
+            trs.append(RemoteDMATransfer(dst_ids=_ids(topo, core, dc), dma_engine_mask=om, remote_sem=asem,
+                                         srcs=[src], dsts=[slot(T, rank, d) for d in direct], alu_op=0))
+        g.remote_dma_fused(trs, local_sem=sem.ls)
+        return (_count(cm) if helpers else 0) + (_count(om) if direct else 0)
 
     left = 0
-    dc = [cores[d] for d in direct]
-    qwait(g, [i_d])
-    if helpers:
-        left += _send(g, topo, core, [(D[:, W:W + 4], [T.RL1[:, 0, :] for h in helpers]),
-                                      (D[:, 0:4], [T.RL1[:, 1, :] for h in helpers])], helpers, sem.h1, sem.ls)
-    if direct:
-        left += _send(g, topo, core, _m1(T, D[:, W:W + 4], D[:, 0:4], rank, direct), dc, sem.a1, sem.ls)
-    qwait(g, [i_pad, i_m, i_s])
-    if helpers:
-        left += _send(g, topo, core, [(R2[:, 0, :], [T.RL2[:] for h in helpers])], helpers, sem.h2, sem.ls)
-    if direct:
-        left += _send(g, topo, core, _m2(T, R2[:, 0, :], rank, direct), dc, sem.a2, sem.ls)
+    need(g, "g", [i_de])
+    left += send(R1[:, 0:M1], T.RL1, sem.h1, _slot1, sem.a1)
+    need(g, "g", [i_s, i_m, f_a])
+    left += send(R2[:, 0:M2], T.RL2, sem.h2, _slot2, sem.a2)
     g.wait_ge(sem.ls, left)
-    g.wait_ge(sem.st, 32)
-    qwait(g, range(n[0] - K, n[0]))
+    g.wait_ge(sem.st, 64)
+    need(g, "g", [i for i in range(nid[0]) if i not in consumed])

@@ -4,27 +4,27 @@ from concourse.mybir import AluOpType, AxisListType, ActivationFunctionType
 
 N = 6
 W = 256
-WI = W - 4
+H = W // 2
+PAD = 8
 NSIM = 256
 NC = 44
-M1 = 8
-M2 = 2
-R2O = 8
+M = 8
 
 F = "float32"
 SCRATCH = {
-    "E": ("sbuf", [128, 2, 12], F),
-    "Q": ("sbuf", [128, 12], F), "HB": ("sbuf", [128, 8], F), "PE": ("sbuf", [128, 11], F),
-    "TE": ("sbuf", [128, 8], F), "AE": ("sbuf", [128, 8], F), "YE": ("sbuf", [128, 8], F),
-    "UB": ("sbuf", [128, W], F), "BB": ("sbuf", [128, W], F),
-    "P": ("sbuf", [128, W], F), "A": ("sbuf", [128, WI], F), "Y8": ("sbuf", [128, WI], F), "D": ("sbuf", [128, WI], F),
-    "SQ": ("sbuf", [128, WI], F), "Y": ("sbuf", [128, WI], F),
-    "U8": ("psum", [128, 512], F), "B4": ("psum", [128, 512], F),
-    "R1": ("sbuf", [128, 7 * M1], F),
-    "R2": ("sbuf", [128, 20], F),
-    "O": ("sbuf", [128, 24], F), "SO2": ("sbuf", [128, 24], F), "MO": ("sbuf", [128, 1], F), "MX": ("sbuf", [128, 1], F),
-    "YR": ("sbuf", [128, 2], F), "YL": ("sbuf", [128, 2], F), "SO": ("sbuf", [128, 2], F),
-    "RL1": ("sbuf", [128, M1], F), "RL2": ("sbuf", [128, M2], F),
+    "XO": ("sbuf", [128, M], F),
+    "BE": ("sbuf", [128, 4], F), "E8": ("sbuf", [128, M], F), "B4E": ("sbuf", [128, 4], F),
+    "MS": ("sbuf", [128, 2, 4], F),
+    "UBP": ("sbuf", [128, W + 2 * PAD], F), "BB": ("sbuf", [128, W], F),
+    "W5": ("sbuf", [128, W + 2], F), "XX": ("sbuf", [128, W], F), "D": ("sbuf", [128, W], F),
+    "SQ": ("sbuf", [128, W], F), "Y8": ("sbuf", [128, W], F), "Y": ("sbuf", [128, W], F),
+    "V9": ("psum", [128, 512], F), "U8": ("psum", [128, 512], F), "B4A": ("psum", [128, 512], F), "B4B": ("psum", [128, 512], F),
+    "X": ("sbuf", [128, 7 * M], F),
+    "PE": ("sbuf", [128, 52], F), "AE": ("sbuf", [128, 6, 8], F),
+    "G": ("sbuf", [128, 14, 4], F),
+    "OT": ("sbuf", [128, 36], F), "ST": ("sbuf", [128, 36], F), "MX": ("sbuf", [128, 1], F),
+    "YE": ("sbuf", [128, 4], F), "SO": ("sbuf", [128, 2], F),
+    "RL1": ("sbuf", [128, M], F), "RL2": ("sbuf", [128, 2, 4], F),
 }
 SEMAPHORES = ["leu", "leb", "lu", "lb", "a1", "a2", "h1", "h2", "ls", "st"] + ["c%d" % i for i in range(NC)]
 
@@ -73,12 +73,12 @@ def _rank_masks(topo, cores, plan, j):
 
 def _slot1(T, j, d):
     k = (j - d) % N
-    return T.R1[:, M1 * k:M1 * k + M1]
+    return T.X[:, M * k:M * k + M]
 
 
 def _slot2(T, j, d):
     k = (j - d) % N
-    return T.R2[:, R2O + M2 * (k - 1):R2O + M2 * k]
+    return T.G[:, 2 * k:2 * k + 2, :]
 
 
 def _carrier(g, core, T, topo, j, share, n_in):
@@ -109,8 +109,8 @@ def rank_program(g, core, T, topo):
     direct, helpers, share = plan[rank]
     sem = T.sem
     add, sub, mul, mx = AluOpType.add, AluOpType.subtract, AluOpType.mult, AluOpType.max
-    X = AxisListType.X
-    Copy, Square = ActivationFunctionType.Copy, ActivationFunctionType.Square
+    AX = AxisListType.X
+    Copy, Square, Ident = ActivationFunctionType.Copy, ActivationFunctionType.Square, ActivationFunctionType.Identity
     vq, sq, yq = g.vector, g.scalar, g.sync
     nid = [0]
     waited = {}
@@ -148,87 +148,100 @@ def rank_program(g, core, T, topo):
                 if rank in s:
                     arrive += _count(_mask(topo, h, [cores[d] for d in s]))
 
-    E, R1, R2, O = T.E, T.R1, T.R2, T.O
-    c1 = 1.0 / math.sqrt(float(N * W))
+    XO, MS, UBP, X, G, AE, PE, OT, ST = T.XO, T.MS, T.UBP, T.X, T.G, T.AE, T.PE, T.OT, T.ST
+    c8 = 1.0 / (8.0 * math.sqrt(float(N * W)))
 
-    yq.dma_start(E[:, 0, 0:4], T.u[:, W - 4:W]).then_inc(sem.leu, 16)
-    sq.dma_start(E[:, 0, 8:12], T.u[:, 0:4]).then_inc(sem.leu, 16)
-    yq.dma_start(E[:, 1, 0:4], T.b[:, W - 4:W]).then_inc(sem.leb, 16)
-    sq.dma_start(E[:, 1, 8:12], T.b[:, 0:4]).then_inc(sem.leb, 16)
-    yq.dma_start(T.UB[0:64, :], T.u[0:64, :]).then_inc(sem.lu, 16)
-    sq.dma_start(T.UB[64:128, :], T.u[64:128, :]).then_inc(sem.lu, 16)
+    yq.dma_start(XO[:, 4:8], T.u[:, W - 4:W]).then_inc(sem.leu, 16)
+    sq.dma_start(XO[:, 0:4], T.u[:, 0:4]).then_inc(sem.leu, 16)
+    yq.dma_start(T.BE[:, 2:4], T.b[:, W - 2:W]).then_inc(sem.leb, 16)
+    sq.dma_start(T.BE[:, 0:2], T.b[:, 0:2]).then_inc(sem.leb, 16)
+    yq.dma_start(UBP[0:64, PAD:PAD + W], T.u[0:64, :]).then_inc(sem.lu, 16)
+    sq.dma_start(UBP[64:128, PAD:PAD + W], T.u[64:128, :]).then_inc(sem.lu, 16)
     yq.dma_start(T.BB[0:64, :], T.b[0:64, :]).then_inc(sem.lb, 16)
     sq.dma_start(T.BB[64:128, :], T.b[64:128, :]).then_inc(sem.lb, 16)
 
-    f_e = done(vq.memset(E[:, :, 4:8], 0.0))
-    f_a = done(vq.memset(R2[:, 2:4], 0.0))
-    f_b = done(vq.memset(R2[:, 5:8], 0.0))
+    f_l = done(vq.memset(UBP[:, 0:PAD], 0.0))
+    f_r = done(vq.memset(UBP[:, PAD + W:2 * PAD + W], 0.0))
 
-    S([f_e])
     sq.wait_ge(sem.leu, 32)
-    i_q = done(sq.activation(T.Q[:], E[:, 0, :], Copy, scale=0.125))
-    V([f_e])
+    i_e8 = done(sq.activation(T.E8[:], XO[:], Copy, scale=8.0))
+    i_x0 = done(sq.activation(X[:, 0:M], XO[:], Copy))
+    i_x6 = done(sq.activation(X[:, 6 * M:7 * M], XO[:], Copy))
     vq.wait_ge(sem.leb, 32)
-    i_hb = done(vq.tensor_scalar(T.HB[:], E[:, 1, 2:10], 0.5, None, mul))
-    V([i_q])
-    i_pe = done(vq.tensor_tensor(T.PE[:], T.Q[:, 0:11], T.Q[:, 1:12], add))
-    V([i_hb])
-    vq.wait_ge(sem.leu, 32)
-    i_te = done(vq.tensor_tensor(T.TE[:], T.HB[:], E[:, 0, 2:10], sub))
-    V([i_pe])
-    i_ae = done(vq.tensor_tensor(T.AE[:], T.PE[:, 0:8], T.PE[:, 3:11], add))
-    V([i_ae, i_te])
-    i_de = done(vq.tensor_tensor(R1[:, 0:M1], T.AE[:], T.TE[:], add))
+    i_b4e = done(vq.tensor_scalar(T.B4E[:], T.BE[:], 4.0, None, mul))
+    V([i_b4e, i_e8])
+    i_tl = done(vq.tensor_tensor(MS[:, 0, 0:2], T.B4E[:, 0:2], T.E8[:, 0:2], sub))
+    i_tr = done(vq.tensor_tensor(MS[:, 1, 0:2], T.B4E[:, 2:4], T.E8[:, 6:8], sub))
 
     sq.wait_ge(sem.lu, 32)
-    i_u8 = done(sq.activation(T.U8[:, 0:WI], T.UB[:, 2:2 + WI], Copy, scale=8.0))
+    i_v9 = done(sq.activation(T.V9[:, 0:W], UBP[:, PAD:PAD + W], Copy, scale=-9.0))
     sq.wait_ge(sem.lb, 32)
-    i_b4 = done(sq.activation(T.B4[:, 0:WI], T.BB[:, 2:2 + WI], Copy, scale=4.0))
+    i_b4a = done(sq.activation(T.B4A[:, 0:H], T.BB[:, 0:H], Copy, scale=4.0))
+    i_b4b = done(sq.activation(T.B4B[:, 0:H], T.BB[:, H:W], Copy, scale=4.0))
     vq.wait_ge(sem.lu, 32)
-    i_p = done(vq.tensor_tensor(T.P[:, 0:W - 1], T.UB[:, 0:W - 1], T.UB[:, 1:W], add))
-    V([i_p])
-    i_a = done(vq.tensor_tensor(T.A[:], T.P[:, 0:WI], T.P[:, 3:3 + WI], add))
-    V([i_a, i_b4])
-    i_y8 = done(vq.tensor_tensor(T.Y8[:], T.A[:], T.B4[:, 0:WI], add))
-    V([i_y8, i_u8])
-    i_d = done(vq.tensor_tensor(T.D[:], T.Y8[:], T.U8[:, 0:WI], sub))
-    V([i_d])
-    i_m = done(vq.tensor_reduce(R2[:, 1:2], T.D[:], X, mx, apply_absolute_value=True))
-    S([i_d])
-    i_s = done(sq.activation(T.SQ[:], T.D[:], Square, scale=c1 / 8.0, accum_out=R2[:, 0:1]))
+    V([f_l, f_r])
+    i_w = done(vq.tensor_tensor_scan(T.W5[:], UBP[:, PAD:PAD + W + 2], UBP[:, PAD - 5:PAD + W - 3], 0.0, add, sub))
+    V([i_w, i_v9])
+    i_xa = done(vq.tensor_tensor(T.XX[:, 0:H], T.W5[:, 2:2 + H], T.V9[:, 0:H], add))
+    i_xb = done(vq.tensor_tensor(T.XX[:, H:W], T.W5[:, 2 + H:2 + W], T.V9[:, H:W], add))
+    V([i_xa, i_b4a])
+    i_da = done(vq.tensor_tensor(T.D[:, 0:H], T.XX[:, 0:H], T.B4A[:, 0:H], add))
+    V([i_xb, i_b4b])
+    i_db = done(vq.tensor_tensor(T.D[:, H:W], T.XX[:, H:W], T.B4B[:, 0:H], add))
+    V([i_da])
+    i_ma = done(vq.tensor_reduce(MS[:, 0, 2:3], T.D[:, 2:H], AX, mx, apply_absolute_value=True))
+    V([i_db])
+    i_mb = done(vq.tensor_reduce(MS[:, 1, 2:3], T.D[:, H:W - 2], AX, mx, apply_absolute_value=True))
+    S([i_da])
+    i_sa = done(sq.activation(T.SQ[:, 2:H], T.D[:, 2:H], Square, scale=c8, accum_out=MS[:, 0, 3:4]))
+    S([i_db])
+    i_sb = done(sq.activation(T.SQ[:, H:W - 2], T.D[:, H:W - 2], Square, scale=c8, accum_out=MS[:, 1, 3:4]))
+
+    i_u8 = done(sq.activation(T.U8[:, 0:W], UBP[:, PAD:PAD + W], Copy, scale=8.0))
+    V([i_u8])
+    i_y8 = done(vq.tensor_tensor(T.Y8[:], T.D[:], T.U8[:, 0:W], add))
     S([i_y8])
     i_y = done(sq.activation(T.Y[:], T.Y8[:], Copy, scale=0.125))
-
-    i_d6 = done(vq.tensor_tensor(R1[:, 6 * M1:7 * M1], T.AE[:], T.TE[:], add))
-    i_ye = done(vq.tensor_tensor(T.YE[:], T.AE[:], T.HB[:], add))
+    V([i_tl, i_tr, i_ma, i_mb, i_sa, i_sb])
+    i_g1 = done(vq.tensor_copy(G[:, 1, :], MS[:, 1, :]))
+    i_g12 = done(vq.tensor_copy(G[:, 12, :], MS[:, 0, :]))
 
     vq.wait_ge(sem.a1, arrive)
-    V([i_de, i_d6])
-    i_o = [done(vq.tensor_tensor(O[:, 6 * j:6 * j + 6], R1[:, j:6 * M1:M1], R1[:, M1 + 4 + j:7 * M1:M1], add))
-           for j in range(4)]
-    V([i_ye])
-    i_yr = done(vq.tensor_tensor(T.YR[:], T.YE[:, 0:2], R1[:, M1 + 4:M1 + 6], add))
-    i_yl = done(vq.tensor_tensor(T.YL[:], T.YE[:, 6:8], R1[:, 5 * M1 + 2:5 * M1 + 4], add))
-    V(i_o)
-    i_mo = done(vq.tensor_reduce(T.MO[:], O[:], X, mx, apply_absolute_value=True))
-    S(i_o + [f_b])
-    i_so = done(sq.activation(T.SO2[:], O[:], Square, scale=c1, accum_out=R2[:, 4:5]))
+    V([i_x0, i_x6])
+    i_pe = done(vq.tensor_tensor(PE[:, 0:51], X[:, 4:55], X[:, 5:56], add))
+    V([i_pe])
+    i_ae = done(vq.tensor_tensor(AE[:, :, :], PE[:, 0:48], PE[:, 3:51], add))
+    sq.wait_ge(sem.a1, arrive)
+    S([i_y])
+    i_e2 = done(sq.activation(T.YE[:, 2:3], X[:, M:M + 1], Ident, bias=T.Y[:, W - 2:W - 1], scale=0.125))
+    i_e1 = done(sq.activation(T.YE[:, 1:2], X[:, 6 * M - 1:6 * M], Ident, bias=T.Y[:, 1:2], scale=0.125))
+    S([i_pe])
+    i_e3 = done(sq.activation(T.YE[:, 3:4], PE[:, 4:5], Ident, bias=T.Y[:, W - 1:W], scale=0.125))
+    i_e0 = done(sq.activation(T.YE[:, 0:1], PE[:, 42:43], Ident, bias=T.Y[:, 0:1], scale=0.125))
 
     vq.wait_ge(sem.a2, arrive)
-    V([i_m, f_a, f_b])
-    i_f1 = done(vq.tensor_reduce(T.MX[:], R2[:, 1:R2O + 5 * M2:2], X, mx))
-    V([i_s, i_so])
-    i_f2 = done(vq.tensor_reduce(T.SO[:, 0:1], R2[:, 0:R2O + 5 * M2:2], X, add))
-    V([i_f1, i_mo])
-    i_f3 = done(vq.tensor_scalar(T.SO[:, 1:2], T.MX[:], 0.125, T.MO[:], mul, mx))
+    V([i_g1, i_g12, i_ae])
+    i_a = done(vq.tensor_tensor(OT[:, 0:24], G[:, 1:13, 0:2], AE[:, :, 0:4], add))
+    sq.wait_ge(sem.a2, arrive)
+    S([i_g1, i_g12])
+    i_mc = done(sq.activation(OT[:, 24:36], G[:, 1:13, 2], Copy))
+    i_sc = done(sq.activation(ST[:, 24:36], G[:, 1:13, 3], Copy))
+    S([i_a])
+    i_sq = done(sq.activation(ST[:, 0:24], OT[:, 0:24], Square, scale=c8))
+    V([i_a, i_mc])
+    i_mx = done(vq.tensor_reduce(T.MX[:], OT[:], AX, mx, apply_absolute_value=True))
+    V([i_sq, i_sc])
+    i_f0 = done(vq.tensor_reduce(T.SO[:, 0:1], ST[:], AX, add))
+    S([i_mx])
+    i_f1 = done(sq.activation(T.SO[:, 1:2], T.MX[:], Copy, scale=0.125))
 
     need(yq, "y", [i_y])
-    yq.dma_start(T.y[:, 2:2 + WI], T.Y[:]).then_inc(sem.st, 16)
-    need(yq, "y", [i_yr])
-    yq.dma_start(T.y[:, W - 2:W], T.YR[:]).then_inc(sem.st, 16)
-    S([i_yl])
-    sq.dma_start(T.y[:, 0:2], T.YL[:]).then_inc(sem.st, 16)
-    need(yq, "y", [i_f2, i_f3])
+    yq.dma_start(T.y[:, 2:W - 2], T.Y[:, 2:W - 2]).then_inc(sem.st, 16)
+    need(yq, "y", [i_e2, i_e3])
+    yq.dma_start(T.y[:, W - 2:W], T.YE[:, 2:4]).then_inc(sem.st, 16)
+    need(yq, "y", [i_e0, i_e1])
+    yq.dma_start(T.y[:, 0:2], T.YE[:, 0:2]).then_inc(sem.st, 16)
+    need(yq, "y", [i_f0, i_f1])
     yq.dma_start(T.s[:], T.SO[:]).then_inc(sem.st, 16)
 
     cm, om = _rank_masks(topo, cores, plan, rank)
@@ -246,10 +259,10 @@ def rank_program(g, core, T, topo):
         return (_count(cm) if helpers else 0) + (_count(om) if direct else 0)
 
     left = 0
-    need(g, "g", [i_de])
-    left += send(R1[:, 0:M1], T.RL1, sem.h1, _slot1, sem.a1)
-    need(g, "g", [i_s, i_m, f_a])
-    left += send(R2[:, 0:M2], T.RL2, sem.h2, _slot2, sem.a2)
+    g.wait_ge(sem.leu, 32)
+    left += send(XO[:], T.RL1, sem.h1, _slot1, sem.a1)
+    need(g, "g", [i_tl, i_tr, i_ma, i_mb, i_sa, i_sb])
+    left += send(MS[:], T.RL2, sem.h2, _slot2, sem.a2)
     g.wait_ge(sem.ls, left)
     g.wait_ge(sem.st, 64)
     need(g, "g", [i for i in range(nid[0]) if i not in consumed])

import math
from concourse.bass import DstId, RemoteDMATransfer
from concourse.mybir import AluOpType, AxisListType, ActivationFunctionType

N = 6
W = 256
H = W // 2
PAD = 8
NSIM = 256
NC = 44
M = 8

F = "float32"
SCRATCH = {
    "XO": ("sbuf", [128, M], F),
    "BE": ("sbuf", [128, 4], F), "E8": ("sbuf", [128, M], F), "B4E": ("sbuf", [128, 4], F),
    "MS": ("sbuf", [128, 2, 4], F),
    "UBP": ("sbuf", [128, W + 2 * PAD], F), "BB": ("sbuf", [128, W], F),
    "W5": ("sbuf", [128, W + 2], F), "XX": ("sbuf", [128, W], F), "D": ("sbuf", [128, W], F),
    "SQ": ("sbuf", [128, W], F), "Y8": ("sbuf", [128, W], F), "Y": ("sbuf", [128, W], F),
    "V9": ("psum", [128, 512], F), "U8": ("psum", [128, 512], F), "B4A": ("psum", [128, 512], F), "B4B": ("psum", [128, 512], F),
    "X": ("sbuf", [128, 7 * M], F),
    "PE": ("sbuf", [128, 52], F), "AE": ("sbuf", [128, 6, 8], F),
    "G": ("sbuf", [128, 14, 4], F),
    "OT": ("sbuf", [128, 36], F), "ST": ("sbuf", [128, 36], F), "MX": ("sbuf", [128, 1], F),
    "YE": ("sbuf", [128, 4], F), "SO": ("sbuf", [128, 2], F),
    "RL1": ("sbuf", [128, M], F), "RL2": ("sbuf", [128, 2, 4], F),
}
SEMAPHORES = ["leu", "leb", "lu", "lb", "a1", "a2", "h1", "h2", "ls", "st"] + ["c%d" % i for i in range(NC)]


def _plan(T, topo):
    cores = list(T.cores)
    plan = []
    for j, c in enumerate(cores):
        others = [(j + k) % N for k in range(1, N)]
        direct = [d for d in others if topo.may_write(c, cores[d])]
        far = [d for d in others if not topo.may_write(c, cores[d])]
        helpers = [x for x in range(NSIM)
                   if far and x not in cores and topo.host(x) == topo.host(c) and topo.chip(x) == topo.chip(c)
                   and topo.die(x) == topo.die(c) and all(topo.may_write(x, cores[d]) for d in far)]
        helpers = helpers[:min(2, len(far))]
        share = [far[i::len(helpers)] for i in range(len(helpers))]
        plan.append((direct, helpers, share))
    return plan


def _mask(topo, src, dsts):
    m = topo.mask(src, dsts[0])
    for d in dsts[1:]:
        m &= topo.mask(src, d)
    return m


def _count(m):
    return bin(m).count("1")


def _ids(topo, src, dsts):
    out = []
    for d in dsts:
        rid, pid = topo.addr(d, src)
        out.append(DstId(rid=rid, pnc=pid))
    return out


def _rank_masks(topo, cores, plan, j):
    direct, helpers, share = plan[j]
    off = _mask(topo, cores[j], [cores[d] for d in direct]) if direct else 0
    on = _mask(topo, cores[j], helpers) if helpers else 0
    return on & ~off, off


def _slot1(T, j, d):
    k = (j - d) % N
    return T.X[:, M * k:M * k + M]


def _slot2(T, j, d):
    k = (j - d) % N
    return T.G[:, 2 * k:2 * k + 2, :]


def _carrier(g, core, T, topo, j, share, n_in):
    cores = list(T.cores)
    dsts = [cores[d] for d in share]
    m = _mask(topo, core, dsts)
    ids = _ids(topo, core, dsts)
    g.wait_ge(T.sem.h1, n_in)
    g.remote_dma_fused([RemoteDMATransfer(dst_ids=ids, dma_engine_mask=m, remote_sem=T.sem.a1, srcs=[T.RL1[:]],
                                          dsts=[_slot1(T, j, d) for d in share], alu_op=0)], local_sem=T.sem.ls)
    g.wait_ge(T.sem.h2, n_in)
    g.remote_dma_fused([RemoteDMATransfer(dst_ids=ids, dma_engine_mask=m, remote_sem=T.sem.a2, srcs=[T.RL2[:]],
                                          dsts=[_slot2(T, j, d) for d in share], alu_op=0)], local_sem=T.sem.ls)
    g.wait_ge(T.sem.ls, 2 * _count(m))


def rank_program(g, core, T, topo):
    plan = _plan(T, topo)
    cores = list(T.cores)
    rank = T.rank_of(core)
    if rank is None:
        for j in range(N):
            direct, helpers, share = plan[j]
            if core in helpers:
                _carrier(g, core, T, topo, j, share[helpers.index(core)], _count(_rank_masks(topo, cores, plan, j)[0]))
        return

    direct, helpers, share = plan[rank]
    sem = T.sem
    add, sub, mul, mx = AluOpType.add, AluOpType.subtract, AluOpType.mult, AluOpType.max
    AX = AxisListType.X
    Copy, Square, Ident = ActivationFunctionType.Copy, ActivationFunctionType.Square, ActivationFunctionType.Identity
    vq, sq, yq = g.vector, g.scalar, g.sync
    nid = [0]
    waited = {}
    consumed = set()

    def need(q, name, ids):
        seen = waited.setdefault(name, set())
        for i in ids:
            if i not in seen:
                q.wait_ge(sem["c%d" % i], 1)
                seen.add(i)
                consumed.add(i)

    def done(instr):
        i = nid[0]
        instr.then_inc(sem["c%d" % i], 1)
        nid[0] += 1
        return i

    def V(ids):
        need(vq, "v", ids)

    def S(ids):
        need(sq, "s", ids)

    arrive = 0
    for j in range(N):
        if j == rank:
            continue
        dj, hj, sj = plan[j]
        if rank in dj:
            arrive += _count(_rank_masks(topo, cores, plan, j)[1])
        else:
            for h, s in zip(hj, sj):
                if rank in s:
                    arrive += _count(_mask(topo, h, [cores[d] for d in s]))

    XO, MS, UBP, X, G, AE, PE, OT, ST = T.XO, T.MS, T.UBP, T.X, T.G, T.AE, T.PE, T.OT, T.ST
    c8 = 1.0 / (8.0 * math.sqrt(float(N * W)))

    yq.dma_start(XO[:, 4:8], T.u[:, W - 4:W]).then_inc(sem.leu, 16)
    sq.dma_start(XO[:, 0:4], T.u[:, 0:4]).then_inc(sem.leu, 16)
    yq.dma_start(T.BE[:, 2:4], T.b[:, W - 2:W]).then_inc(sem.leb, 16)
    sq.dma_start(T.BE[:, 0:2], T.b[:, 0:2]).then_inc(sem.leb, 16)
    yq.dma_start(UBP[0:64, PAD:PAD + W], T.u[0:64, :]).then_inc(sem.lu, 16)
    sq.dma_start(UBP[64:128, PAD:PAD + W], T.u[64:128, :]).then_inc(sem.lu, 16)
    yq.dma_start(T.BB[0:64, :], T.b[0:64, :]).then_inc(sem.lb, 16)
    sq.dma_start(T.BB[64:128, :], T.b[64:128, :]).then_inc(sem.lb, 16)

    f_l = done(vq.memset(UBP[:, 0:PAD], 0.0))
    f_r = done(vq.memset(UBP[:, PAD + W:2 * PAD + W], 0.0))

    sq.wait_ge(sem.leu, 32)
    i_e8 = done(sq.activation(T.E8[:], XO[:], Copy, scale=8.0))
    i_x0 = done(sq.activation(X[:, 0:M], XO[:], Copy))
    i_x6 = done(sq.activation(X[:, 6 * M:7 * M], XO[:], Copy))
    vq.wait_ge(sem.leb, 32)
    i_b4e = done(vq.tensor_scalar(T.B4E[:], T.BE[:], 4.0, None, mul))
    V([i_b4e, i_e8])
    i_tl = done(vq.tensor_tensor(MS[:, 0, 0:2], T.B4E[:, 0:2], T.E8[:, 0:2], sub))
    i_tr = done(vq.tensor_tensor(MS[:, 1, 0:2], T.B4E[:, 2:4], T.E8[:, 6:8], sub))

    sq.wait_ge(sem.lu, 32)
    i_v9 = done(sq.activation(T.V9[:, 0:W], UBP[:, PAD:PAD + W], Copy, scale=-9.0))
    sq.wait_ge(sem.lb, 32)
    i_b4a = done(sq.activation(T.B4A[:, 0:H], T.BB[:, 0:H], Copy, scale=4.0))
    i_b4b = done(sq.activation(T.B4B[:, 0:H], T.BB[:, H:W], Copy, scale=4.0))
    vq.wait_ge(sem.lu, 32)
    V([f_l, f_r])
    i_w = done(vq.tensor_tensor_scan(T.W5[:], UBP[:, PAD:PAD + W + 2], UBP[:, PAD - 5:PAD + W - 3], 0.0, add, sub))
    V([i_w, i_v9])
    i_xa = done(vq.tensor_tensor(T.XX[:, 0:H], T.W5[:, 2:2 + H], T.V9[:, 0:H], add))
    i_xb = done(vq.tensor_tensor(T.XX[:, H:W], T.W5[:, 2 + H:2 + W], T.V9[:, H:W], add))
    V([i_xa, i_b4a])
    i_da = done(vq.tensor_tensor(T.D[:, 0:H], T.XX[:, 0:H], T.B4A[:, 0:H], add))
    V([i_xb, i_b4b])
    i_db = done(vq.tensor_tensor(T.D[:, H:W], T.XX[:, H:W], T.B4B[:, 0:H], add))
    V([i_da])
    i_ma = done(vq.tensor_reduce(MS[:, 0, 2:3], T.D[:, 2:H], AX, mx, apply_absolute_value=True))
    V([i_db])
    i_mb = done(vq.tensor_reduce(MS[:, 1, 2:3], T.D[:, H:W - 2], AX, mx, apply_absolute_value=True))
    S([i_da])
    i_sa = done(sq.activation(T.SQ[:, 2:H], T.D[:, 2:H], Square, scale=c8, accum_out=MS[:, 0, 3:4]))
    S([i_db])
    i_sb = done(sq.activation(T.SQ[:, H:W - 2], T.D[:, H:W - 2], Square, scale=c8, accum_out=MS[:, 1, 3:4]))

    i_u8 = done(sq.activation(T.U8[:, 0:W], UBP[:, PAD:PAD + W], Copy, scale=8.0))
    V([i_u8])
    i_y8 = done(vq.tensor_tensor(T.Y8[:], T.D[:], T.U8[:, 0:W], add))
    S([i_y8])
    i_y = done(sq.activation(T.Y[:], T.Y8[:], Copy, scale=0.125))
    V([i_tl, i_tr, i_ma, i_mb, i_sa, i_sb])
    i_g1 = done(vq.tensor_copy(G[:, 1, :], MS[:, 1, :]))
    i_g12 = done(vq.tensor_copy(G[:, 12, :], MS[:, 0, :]))

    vq.wait_ge(sem.a1, arrive)
    V([i_x0, i_x6])
    i_pe = done(vq.tensor_tensor(PE[:, 0:51], X[:, 4:55], X[:, 5:56], add))
    V([i_pe])
    i_ae = done(vq.tensor_tensor(AE[:, :, :], PE[:, 0:48], PE[:, 3:51], add))
    sq.wait_ge(sem.a1, arrive)
    S([i_y])
    i_e2 = done(sq.activation(T.YE[:, 2:3], X[:, M:M + 1], Ident, bias=T.Y[:, W - 2:W - 1], scale=0.125))
    i_e1 = done(sq.activation(T.YE[:, 1:2], X[:, 6 * M - 1:6 * M], Ident, bias=T.Y[:, 1:2], scale=0.125))
    S([i_pe])
    i_e3 = done(sq.activation(T.YE[:, 3:4], PE[:, 4:5], Ident, bias=T.Y[:, W - 1:W], scale=0.125))
    i_e0 = done(sq.activation(T.YE[:, 0:1], PE[:, 42:43], Ident, bias=T.Y[:, 0:1], scale=0.125))

    vq.wait_ge(sem.a2, arrive)
    V([i_g1, i_g12, i_ae])
    i_a = done(vq.tensor_tensor(OT[:, 0:24], G[:, 1:13, 0:2], AE[:, :, 0:4], add))
    sq.wait_ge(sem.a2, arrive)
    S([i_g1, i_g12])
    i_mc = done(sq.activation(OT[:, 24:36], G[:, 1:13, 2], Copy))
    i_sc = done(sq.activation(ST[:, 24:36], G[:, 1:13, 3], Copy))
    S([i_a])
    i_sq = done(sq.activation(ST[:, 0:24], OT[:, 0:24], Square, scale=c8))
    V([i_a, i_mc])
    i_mx = done(vq.tensor_reduce(T.MX[:], OT[:], AX, mx, apply_absolute_value=True))
    V([i_sq, i_sc])
    i_f0 = done(vq.tensor_reduce(T.SO[:, 0:1], ST[:], AX, add))
    S([i_mx])
    i_f1 = done(sq.activation(T.SO[:, 1:2], T.MX[:], Copy, scale=0.125))

    need(yq, "y", [i_y])
    yq.dma_start(T.y[:, 2:W - 2], T.Y[:, 2:W - 2]).then_inc(sem.st, 16)
    need(yq, "y", [i_e2, i_e3])
    yq.dma_start(T.y[:, W - 2:W], T.YE[:, 2:4]).then_inc(sem.st, 16)
    need(yq, "y", [i_e0, i_e1])
    yq.dma_start(T.y[:, 0:2], T.YE[:, 0:2]).then_inc(sem.st, 16)
    need(yq, "y", [i_f0, i_f1])
    yq.dma_start(T.s[:], T.SO[:]).then_inc(sem.st, 16)

    cm, om = _rank_masks(topo, cores, plan, rank)
    dc = [cores[d] for d in direct]

    def send(src, hbuf, hsem, slot, asem):
        trs = []
        if helpers:
            trs.append(RemoteDMATransfer(dst_ids=_ids(topo, core, helpers), dma_engine_mask=cm, remote_sem=hsem,
                                         srcs=[src], dsts=[hbuf[:] for h in helpers], alu_op=0))
        if direct:
            trs.append(RemoteDMATransfer(dst_ids=_ids(topo, core, dc), dma_engine_mask=om, remote_sem=asem,
                                         srcs=[src], dsts=[slot(T, rank, d) for d in direct], alu_op=0))
        g.remote_dma_fused(trs, local_sem=sem.ls)
        return (_count(cm) if helpers else 0) + (_count(om) if direct else 0)

    left = 0
    g.wait_ge(sem.leu, 32)
    left += send(XO[:], T.RL1, sem.h1, _slot1, sem.a1)
    need(g, "g", [i_tl, i_tr, i_ma, i_mb, i_sa, i_sb])
    left += send(MS[:], T.RL2, sem.h2, _slot2, sem.a2)
    g.wait_ge(sem.ls, left)
    g.wait_ge(sem.st, 64)
    need(g, "g", [i for i in range(nid[0]) if i not in consumed])
